import numpy as np
import ml_dtypes


def mxq(x, axis, fmt="e4m3"):
    dtype, down = {"e4m3": (ml_dtypes.float8_e4m3fn, 7), "e5m2": (ml_dtypes.float8_e5m2, 14)}[fmt]
    v = np.moveaxis(np.asarray(x, np.float32).astype(ml_dtypes.bfloat16).astype(np.float64), axis, -1)
    blocks = v.reshape(v.shape[:-1] + (-1, 32))
    amax = np.abs(blocks).max(-1, keepdims=True)
    byte = np.maximum(np.where(amax > 0, np.frexp(amax)[1] - 1 + 127, 0) - down, 1)
    scale = np.exp2(byte - 127.0)
    codes = (blocks / scale).astype(np.float32).astype(dtype).astype(np.float64)
    return np.moveaxis((codes * scale).reshape(v.shape), -1, axis)


WIDE = False


def mx_kscale(k):
    if not WIDE:
        return np.ones(k)
    levels = np.array([10, -10, 5, -5, 0])
    if k % 512:
        return np.exp2(np.random.permutation(np.resize(levels, k // 32))).repeat(32)
    a = np.empty((k // 512, 16))
    for p in range(k // 512):
        a[p, :8] = np.random.permutation(np.resize(levels, 8))
        for g in range(8):
            far = levels[np.abs(levels - a[p, g]) >= 10]
            a[p, g + 8] = far[np.random.randint(len(far))]
    return np.exp2(a.ravel()).repeat(32)


def f64(x):
    return np.asarray(x).astype(np.float64)


def striped(idx):
    return np.tile(idx.reshape(-1, 16).T, (8, 1)).astype(np.uint16)


def unstriped(offs):
    return offs[:16].T.reshape(-1).astype(np.int64)


def pack_weight(w):
    k, n = w.shape
    w = f64(np.asarray(w, np.float32).astype(ml_dtypes.bfloat16)).reshape(k // 32, 32, n)
    amax = np.abs(w).max(1)
    byte = np.clip(np.where(amax > 0, np.frexp(amax)[1] - 1 + 127 - 7, 1), 1, 254)
    scaled = (w * np.exp2(127.0 - byte)[:, None, :]).reshape(k, n).astype(np.float32)
    words = np.ascontiguousarray(scaled.reshape(k // 512, 128, 4, n).transpose(0, 1, 3, 2)).astype(ml_dtypes.float8_e4m3fn).view(np.uint8)
    return words, np.ascontiguousarray(byte.astype(np.uint8).reshape(k // 512, 16, n))


def unpack_weight(words, scales):
    g, p, n, _ = words.shape
    vals = np.ascontiguousarray(words).view(ml_dtypes.float8_e4m3fn).astype(np.float64) * np.repeat(np.exp2(scales.astype(np.float64) - 127.0), 8, axis=1)[..., None]
    return vals.transpose(0, 1, 3, 2).reshape(g * 512, n)


def relu(v):
    return np.maximum(v, 0.0)


K, T, S, H, N, D, V, U = 1024, 2048, 512, 512, 256, 2, 256, 512


def setup_inputs():
    n = np.random.standard_normal
    s = mx_kscale(K)[:, None]
    u = mx_kscale(H)
    packed_xT = pack_weight(n((K, T)) * s)
    return {
        "x_words": packed_xT[0],
        "x_scales": packed_xT[1],
        "w1": (n((K, H)) / np.sqrt(K) / s * u).astype(np.float32),
        "w2": (n((H, N)) / np.sqrt(H) / u[:, None]).astype(np.float32),
        "w3": (n((K, N)) / np.sqrt(K) / s).astype(np.float32),
        "offs": striped(np.random.permutation(T)[:S]),
        "tgt": striped(np.random.permutation(T)[:U]),
        "task": striped(np.random.permutation(np.concatenate([np.arange(V), np.random.randint(0, V, U - V)]))),
    }


def reference(x_words, x_scales, w1, w2, w3, offs, tgt, task):
    xq = unpack_weight(x_words, x_scales)[:, unstriped(offs)]
    h = relu(mxq(f64(w1), 0, "e4m3").T @ xq)
    z = h.reshape(len(h), -1, D).mean(axis=2)
    rr = mxq(f64(w2), 0, "e4m3").T @ mxq(z, 0, "e4m3")
    x_tgt = unpack_weight(x_words, x_scales)[:, unstriped(tgt)]
    y = mxq(f64(w3), 0, "e4m3").T @ x_tgt
    return np.tanh(rr[:, unstriped(task)] + y)

@@ -1,0 +1,186 @@
+from contextlib import ExitStack
+
+import concourse.mybir as mybir
+
+K, T, S, H, N, D, V, U = 1024, 2048, 512, 512, 256, 2, 256, 512
+FLOPS = 2 * (K * H * S + H * N * V + K * N * U)
+
+F32 = mybir.dt.float32
+BF16 = mybir.dt.bfloat16
+I32 = mybir.dt.int32
+U32 = mybir.dt.uint32
+U16 = mybir.dt.uint16
+U8 = mybir.dt.uint8
+FP8X4 = mybir.dt.float8_e4m3fn_x4
+ACT = mybir.ActivationFunctionType
+ALU = mybir.AluOpType
+
+P = 128
+PACK = 4
+K_PASS = P * PACK
+PASSES = K // K_PASS
+M_TILES = N // P
+RR_WINDOW = V + 32
+PIECE = 256
+HEAD = 1024
+
+
+def tile_picked_ycnp_tanh_p_kernel(
+    tc, x_words, x_scales, w1, w2, w3, offs, tgt, task, out
+):
+    nc = tc.nc
+    with ExitStack() as ctx:
+        sb = ctx.enter_context(tc.tile_pool(name="sb", bufs=1))
+        ps = ctx.enter_context(tc.psum_pool(name="ps", bufs=1))
+
+        def tile(shape, dtype, name, tag=None):
+            return sb.tile(shape, dtype, name=name, tag=tag or name, align_bytes=64)
+
+        offs_sb = tile([P, S // 16], U16, "offs_sb")
+        tgt_sb = tile([P, U // 16], U16, "tgt_sb")
+        task_sb = tile([P, U // 16], U16, "task_sb")
+        xs = tile([P, T], U8, "xs")
+        xw = [tile([P, T], U32, "xw%d" % g) for g in range(PASSES)]
+        w1_raw = [tile([P, PACK, H], F32, "w1_raw%d" % g) for g in range(PASSES)]
+        w2_raw = tile([P, PACK, N], F32, "w2_raw")
+        w3_raw = [tile([P, PACK, N], F32, "w3_raw%d" % g) for g in range(PASSES)]
+
+
+        def load_words(g, c0, c1):
+            words = x_words[g].rearrange("p c r -> p (c r)").bitcast(I32)
+            nc.sync.dma_start(xw[g][:, c0:c1].bitcast(I32), words[:, c0:c1])
+
+        def load_rows(raw, w, g):
+            nc.sync.dma_start(raw[:], w[g * K_PASS : (g + 1) * K_PASS, :].rearrange("(p j) c -> p j c", j=PACK))
+
+        nc.vector.memset(xs[:].bitcast(I32), 0)
+        nc.sync.dma_start(offs_sb[:], offs)
+        load_words(0, 0, HEAD)
+        nc.sync.dma_start(tgt_sb[:], tgt)
+        for q in range(4):
+            nc.sync.dma_start(xs[32 * q : 32 * q + 8, :].bitcast(I32), x_scales[:, 4 * q : 4 * q + 4, :].bitcast(I32))
+        load_words(0, HEAD, T)
+        load_words(1, 0, T)
+        load_rows(w1_raw[0], w1, 0)
+        load_rows(w1_raw[1], w1, 1)
+        load_rows(w2_raw, w2, 0)
+        for g in range(PASSES):
+            load_rows(w3_raw[g], w3, g)
+        nc.sync.dma_start(task_sb[:], task)
+
+        def gathered(window, offsets, dtype, name, tag=None):
+            picked = tile([P, S], dtype, name, tag)
+            nc.vector.tensor_copy(picked[:], window[:].indirect(offsets[:]))
+            return picked
+
+        ctx_scales = gathered(xs, offs_sb, U8, "ctx_scales")
+        tgt_scales = gathered(xs, tgt_sb, U8, "tgt_scales")
+        ctx_words, tgt_words = [], []
+        for g in range(PASSES):
+            ctx_words.append(gathered(xw[g], offs_sb, U32, "ctx_words%d" % g))
+            tgt_words.append(gathered(xw[g], tgt_sb, U32, "tgt_words%d" % g))
+
+        def cast(engine, dst, src):
+            if engine == "scalar":
+                nc.scalar.activation(dst, src, ACT.Copy)
+            else:
+                nc.vector.tensor_copy(dst, src)
+
+        def quantized(grouped, width, name, tag=None):
+            codes = tile([P, width], U32, name + "_codes", tag)
+            scales = tile([P, width], U8, name + "_scales")
+            nc.vector.quantize_mx(out=codes[:].bitcast(FP8X4), scales=scales[:], in_=grouped)
+            return codes, scales
+
+        h_ps = [ps.tile([P, S], F32, name="h_ps%d" % t) for t in range(PACK)]
+        for g in range(PASSES):
+            src = w1_raw[g][:].rearrange("p j (m t) -> p m j t", t=PACK)
+            for u, engine in enumerate(("vector" if g else "scalar", "scalar")):
+                grouped = tile([P, 2, P, PACK], BF16, "w1_bf%d_%d" % (g, u), "w1_bf0_0" if u == 0 else None)
+                cast(engine, grouped[:].rearrange("p t m j -> p m j t"), src[:, :, :, 2 * u : 2 * u + 2])
+                rows = grouped[:].rearrange("p t m j -> p (t m j)")
+                codes, scales = quantized(rows, 2 * P, "w1_%d_%d" % (g, u))
+                for e in range(2):
+                    nc.tensor.matmul_mx(
+                        out=h_ps[2 * u + e][:],
+                        lhsT=codes[:, e * P : (e + 1) * P].bitcast(FP8X4),
+                        lhsT_scale=scales[:, e * P : (e + 1) * P],
+                        rhs=ctx_words[g][:].bitcast(FP8X4),
+                        rhs_scale=ctx_scales[4 * g :, :],
+                        start=(g == 0),
+                        stop=(g == PASSES - 1),
+                    )
+
+        def interleaved(engine, raw, dtype_name, tag=None):
+            width = raw.shape[2]
+            grouped = tile([P, width, PACK], BF16, dtype_name, tag)
+            cast(
+                engine,
+                grouped[:].rearrange("p (c i) j -> p c j i", i=4),
+                raw.rearrange("p j (c i) -> p c j i", i=4),
+            )
+            return grouped[:].rearrange("p c j -> p (c j)")
+
+        w2_codes, w2_scales = quantized(interleaved("scalar", w2_raw[:], "w2_bf"), N, "w2")
+        z_planes = tile([P, PACK, V], BF16, "z_planes")
+        for t in range(PACK):
+            pairs = h_ps[t][:].rearrange("p (v d) -> p d v", d=D)
+            odd = tile([P, V], F32, "odd%d" % t)
+            nc.scalar.activation(odd[:], pairs[:, 1], ACT.Relu)
+            step = V if t < PACK - 1 else V // 2
+            for v0 in range(0, V, step):
+                vs = slice(v0, v0 + step)
+                nc.vector.scalar_tensor_tensor(z_planes[:, t, vs], pairs[:, 0, vs], 0.0, odd[:, vs], ALU.max, ALU.add)
+        z_bf = [interleaved("vector", z_planes[:, :, v0 : v0 + P], "z_bf%d" % v0) for v0 in range(0, V, P)]
+        z_q = [quantized(z_bf[i], P, "z%d" % i) for i in range(V // P)]
+
+        w3_bf = [interleaved("scalar", w3_raw[g][:], "w3_bf%d" % g, "odd%d" % (2 + g)) for g in range(PASSES)]
+        w3_q = [quantized(w3_bf[0], N, "w3_0", "z_bf%d" % P)]
+        rr = []
+
+        for m in range(M_TILES):
+            cols = slice(m * P, (m + 1) * P)
+            rr_ps = ps.tile([P, V], F32, name="rr_ps%d" % m)
+            for i, (codes, scales) in enumerate(z_q):
+                nc.tensor.matmul_mx(
+                    out=rr_ps[:, i * P : (i + 1) * P],
+                    lhsT=w2_codes[:, cols].bitcast(FP8X4),
+                    lhsT_scale=w2_scales[:, cols],
+                    rhs=codes[:].bitcast(FP8X4),
+                    rhs_scale=scales[:],
+                    start=True,
+                    stop=True,
+                )
+            rr.append(tile([P, RR_WINDOW], F32, "rr%d" % m, "w3_raw1" if m else None))
+            nc.gpsimd.memset(rr[m][:, V:], 0.0)
+            if m == 0:
+                nc.vector.tensor_scalar(rr[m][:, :V], rr_ps[:], 1.0 / D, None, ALU.mult)
+            else:
+                nc.scalar.activation(rr[m][:, :V], rr_ps[:], ACT.Copy, scale=1.0 / D)
+
+        w3_q.append(quantized(w3_bf[1], N, "w3_1", "z1_codes"))
+        y_ps = [ps.tile([P, U], F32, name="y_ps%d" % m) for m in range(M_TILES)]
+        for g in range(PASSES):
+            for m in range(M_TILES):
+                cols = slice(m * P, (m + 1) * P)
+                codes, scales = w3_q[g]
+                nc.tensor.matmul_mx(
+                    out=y_ps[m][:],
+                    lhsT=codes[:, cols].bitcast(FP8X4),
+                    lhsT_scale=scales[:, cols],
+                    rhs=tgt_words[g][:].bitcast(FP8X4),
+                    rhs_scale=tgt_scales[4 * g :, :],
+                    start=(g == 0),
+                    stop=(g == PASSES - 1),
+                )
+
+        for m in range(M_TILES):
+            for r0 in range(0, U, PIECE):
+                name = "%d_%d" % (m, r0)
+                fetched = tile([P, PIECE], F32, "fetched" + name, "odd3" if (m, r0) == (0, 0) else None)
+                nc.vector.tensor_copy(fetched[:], rr[m][:].indirect(task_sb[:, r0 // 16 : (r0 + PIECE) // 16]))
+                summed = tile([P, PIECE], F32, "summed" + name)
+                nc.vector.tensor_tensor(summed[:], fetched[:], y_ps[m][:, r0 : r0 + PIECE], ALU.add)
+                result = tile([P, PIECE], F32, "result" + name)
+                nc.scalar.activation(result[:], summed[:], ACT.Tanh)
+                nc.sync.dma_start(out[m * P : (m + 1) * P, r0 : r0 + PIECE], result[:])

@@ -22,7 +22,6 @@ PASSES = K // K_PASS
 M_TILES = N // P
 RR_WINDOW = V + 32
 PIECE = 256
-HEAD = 1024
 
 
 def tile_picked_ycnp_tanh_p_kernel(
@@ -41,44 +40,45 @@ def tile_picked_ycnp_tanh_p_kernel(
         task_sb = tile([P, U // 16], U16, "task_sb")
         xs = tile([P, T], U8, "xs")
         xw = [tile([P, T], U32, "xw%d" % g) for g in range(PASSES)]
-        w1_raw = [tile([P, PACK, H], F32, "w1_raw%d" % g) for g in range(PASSES)]
-        w2_raw = tile([P, PACK, N], F32, "w2_raw")
-        w3_raw = [tile([P, PACK, N], F32, "w3_raw%d" % g) for g in range(PASSES)]
 
 
-        def load_words(g, c0, c1):
-            words = x_words[g].rearrange("p c r -> p (c r)").bitcast(I32)
-            nc.sync.dma_start(xw[g][:, c0:c1].bitcast(I32), words[:, c0:c1])
-
-        def load_rows(raw, w, g):
+        def load_rows(w, g, name, tag=None):
+            raw = tile([P, PACK, w.shape[1]], F32, name, tag)
             nc.sync.dma_start(raw[:], w[g * K_PASS : (g + 1) * K_PASS, :].rearrange("(p j) c -> p j c", j=PACK))
+            return raw
 
-        nc.vector.memset(xs[:].bitcast(I32), 0)
-        nc.sync.dma_start(offs_sb[:], offs)
-        load_words(0, 0, HEAD)
-        nc.sync.dma_start(tgt_sb[:], tgt)
-        for q in range(4):
-            nc.sync.dma_start(xs[32 * q : 32 * q + 8, :].bitcast(I32), x_scales[:, 4 * q : 4 * q + 4, :].bitcast(I32))
-        load_words(0, HEAD, T)
-        load_words(1, 0, T)
-        load_rows(w1_raw[0], w1, 0)
-        load_rows(w1_raw[1], w1, 1)
-        load_rows(w2_raw, w2, 0)
         for g in range(PASSES):
-            load_rows(w3_raw[g], w3, g)
+            rows = x_scales[g].bitcast(I32).rearrange("(q r) c -> r q c", r=4)
+            nc.sync.dma_start(xs[16 * g : 16 * g + 16, :].bitcast(I32), rows)
+        nc.vector.memset(xs[32:64, :].bitcast(I32), 0)
+        nc.vector.memset(xs[64:, :].bitcast(I32), 0)
+        nc.sync.dma_start(offs_sb[:], offs)
+        nc.sync.dma_start(tgt_sb[:], tgt)
+        for g in range(PASSES):
+            nc.sync.dma_start(xw[g][:].bitcast(I32), x_words[g].rearrange("p c r -> p (c r)").bitcast(I32))
+        w1_raw = [load_rows(w1, 0, "w1_raw0")]
         nc.sync.dma_start(task_sb[:], task)
+
+        picked_scales = tile([P, S + U], U8, "picked_scales")
+        planes = tile([P, S + U], U8, "planes")
+        nc.vector.memset(planes[:].bitcast(I32), 0)
+        nc.vector.tensor_copy(picked_scales[:, :S], xs[:].indirect(offs_sb[:]))
+        nc.vector.tensor_copy(picked_scales[:, S:], xs[:].indirect(tgt_sb[:]))
+        for q in range(4):
+            nc.sync.dma_start(planes[32 * q : 32 * q + 8, :].bitcast(I32), picked_scales[q:32:4, :].bitcast(I32))
+        w1_raw.append(load_rows(w1, 1, "w1_raw1", "xs"))
 
         def gathered(window, offsets, dtype, name, tag=None):
             picked = tile([P, S], dtype, name, tag)
             nc.vector.tensor_copy(picked[:], window[:].indirect(offsets[:]))
             return picked
 
-        ctx_scales = gathered(xs, offs_sb, U8, "ctx_scales")
-        tgt_scales = gathered(xs, tgt_sb, U8, "tgt_scales")
         ctx_words, tgt_words = [], []
         for g in range(PASSES):
             ctx_words.append(gathered(xw[g], offs_sb, U32, "ctx_words%d" % g))
             tgt_words.append(gathered(xw[g], tgt_sb, U32, "tgt_words%d" % g))
+        w2_raw = load_rows(w2, 0, "w2_raw", "xw0")
+        w3_raw = [load_rows(w3, 0, "w3_raw0", "picked_scales"), load_rows(w3, 1, "w3_raw1", "xw1")]
 
         def cast(engine, dst, src):
             if engine == "scalar":
@@ -106,7 +106,7 @@ def tile_picked_ycnp_tanh_p_kernel(
                         lhsT=codes[:, e * P : (e + 1) * P].bitcast(FP8X4),
                         lhsT_scale=scales[:, e * P : (e + 1) * P],
                         rhs=ctx_words[g][:].bitcast(FP8X4),
-                        rhs_scale=ctx_scales[4 * g :, :],
+                        rhs_scale=planes[4 * g :, :S],
                         start=(g == 0),
                         stop=(g == PASSES - 1),
                     )
@@ -121,7 +121,7 @@ def tile_picked_ycnp_tanh_p_kernel(
             )
             return grouped[:].rearrange("p c j -> p (c j)")
 
-        w2_codes, w2_scales = quantized(interleaved("scalar", w2_raw[:], "w2_bf"), N, "w2")
+        w2_codes, w2_scales = quantized(interleaved("vector", w2_raw[:], "w2_bf", "w1_bf1_1"), N, "w2")
         z_planes = tile([P, PACK, V], BF16, "z_planes")
         for t in range(PACK):
             pairs = h_ps[t][:].rearrange("p (v d) -> p d v", d=D)
@@ -134,7 +134,7 @@ def tile_picked_ycnp_tanh_p_kernel(
         z_bf = [interleaved("vector", z_planes[:, :, v0 : v0 + P], "z_bf%d" % v0) for v0 in range(0, V, P)]
         z_q = [quantized(z_bf[i], P, "z%d" % i) for i in range(V // P)]
 
-        w3_bf = [interleaved("scalar", w3_raw[g][:], "w3_bf%d" % g, "odd%d" % (2 + g)) for g in range(PASSES)]
+        w3_bf = [interleaved("scalar", w3_raw[g][:], "w3_bf%d" % g, "odd%d" % (1 + g)) for g in range(PASSES)]
         w3_q = [quantized(w3_bf[0], N, "w3_0", "z_bf%d" % P)]
         rr = []
 
@@ -151,7 +151,7 @@ def tile_picked_ycnp_tanh_p_kernel(
                     start=True,
                     stop=True,
                 )
-            rr.append(tile([P, RR_WINDOW], F32, "rr%d" % m, "w3_raw1" if m else None))
+            rr.append(tile([P, RR_WINDOW], F32, "rr%d" % m, "xw1" if m else None))
             nc.gpsimd.memset(rr[m][:, V:], 0.0)
             if m == 0:
                 nc.vector.tensor_scalar(rr[m][:, :V], rr_ps[:], 1.0 / D, None, ALU.mult)
@@ -169,7 +169,7 @@ def tile_picked_ycnp_tanh_p_kernel(
                     lhsT=codes[:, cols].bitcast(FP8X4),
                     lhsT_scale=scales[:, cols],
                     rhs=tgt_words[g][:].bitcast(FP8X4),
-                    rhs_scale=tgt_scales[4 * g :, :],
+                    rhs_scale=planes[4 * g :, S:],
                     start=(g == 0),
                     stop=(g == PASSES - 1),
                 )
@@ -177,10 +177,13 @@ def tile_picked_ycnp_tanh_p_kernel(
         for m in range(M_TILES):
             for r0 in range(0, U, PIECE):
                 name = "%d_%d" % (m, r0)
-                fetched = tile([P, PIECE], F32, "fetched" + name, "odd3" if (m, r0) == (0, 0) else None)
+                fetched = tile([P, PIECE], F32, "fetched" + name, "odd2" if (m, r0) == (1, 0) else None)
                 nc.vector.tensor_copy(fetched[:], rr[m][:].indirect(task_sb[:, r0 // 16 : (r0 + PIECE) // 16]))
-                summed = tile([P, PIECE], F32, "summed" + name)
-                nc.vector.tensor_tensor(summed[:], fetched[:], y_ps[m][:, r0 : r0 + PIECE], ALU.add)
-                result = tile([P, PIECE], F32, "result" + name)
-                nc.scalar.activation(result[:], summed[:], ACT.Tanh)
-                nc.sync.dma_start(out[m * P : (m + 1) * P, r0 : r0 + PIECE], result[:])
+                step = PIECE // 2 if (m, r0) == (M_TILES - 1, U - PIECE) else PIECE
+                for c0 in range(0, PIECE, step):
+                    cols = slice(r0 + c0, r0 + c0 + step)
+                    summed = tile([P, step], F32, "summed%s_%d" % (name, c0))
+                    nc.vector.tensor_tensor(summed[:], fetched[:, c0 : c0 + step], y_ps[m][:, cols], ALU.add)
+                    result = tile([P, step], F32, "result%s_%d" % (name, c0))
+                    nc.scalar.activation(result[:], summed[:], ACT.Tanh)
+                    nc.sync.dma_start(out[m * P : (m + 1) * P, cols], result[:])

@@ -77,8 +77,8 @@ def tile_picked_ycnp_tanh_p_kernel(
         for g in range(PASSES):
             ctx_words.append(gathered(xw[g], offs_sb, U32, "ctx_words%d" % g))
             tgt_words.append(gathered(xw[g], tgt_sb, U32, "tgt_words%d" % g))
-        w2_raw = load_rows(w2, 0, "w2_raw", "xw0")
-        w3_raw = [load_rows(w3, 0, "w3_raw0", "picked_scales"), load_rows(w3, 1, "w3_raw1", "xw1")]
+        w3_raw = [load_rows(w3, 0, "w3_raw0", "xw0")]
+        w2_raw = load_rows(w2, 0, "w2_raw", "picked_scales")
 
         def cast(engine, dst, src):
             if engine == "scalar":
@@ -121,7 +121,9 @@ def tile_picked_ycnp_tanh_p_kernel(
             )
             return grouped[:].rearrange("p c j -> p (c j)")
 
-        w2_codes, w2_scales = quantized(interleaved("vector", w2_raw[:], "w2_bf", "w1_bf1_1"), N, "w2")
+        w3_raw.append(load_rows(w3, 1, "w3_raw1", "w1_raw0"))
+        w3_bf = [interleaved("scalar", w3_raw[0][:], "w3_bf0", "xs")]
+        w2_q = [quantized(interleaved("vector", w2_raw[:, :, :P], "w2_bf0", "w1_bf1_1"), P, "w2_0")]
         z_planes = tile([P, PACK, V], BF16, "z_planes")
         for t in range(PACK):
             pairs = h_ps[t][:].rearrange("p (v d) -> p d v", d=D)
@@ -134,34 +136,30 @@ def tile_picked_ycnp_tanh_p_kernel(
         z_bf = [interleaved("vector", z_planes[:, :, v0 : v0 + P], "z_bf%d" % v0) for v0 in range(0, V, P)]
         z_q = [quantized(z_bf[i], P, "z%d" % i) for i in range(V // P)]
 
-        w3_bf = [interleaved("scalar", w3_raw[g][:], "w3_bf%d" % g, "odd%d" % (1 + g)) for g in range(PASSES)]
-        w3_q = [quantized(w3_bf[0], N, "w3_0", "z_bf%d" % P)]
+        w2_q.append(quantized(interleaved("scalar", w2_raw[:, :, P:], "w2_bf1", "odd1"), P, "w2_1", "z_bf0"))
+        w3_bf.append(interleaved("scalar", w3_raw[1][:], "w3_bf1", "odd2"))
+        w3_q = [quantized(w3_bf[0], N, "w3_0", "z_bf%d" % P), quantized(w3_bf[1], N, "w3_1", "odd1")]
         rr = []
 
         for m in range(M_TILES):
-            cols = slice(m * P, (m + 1) * P)
             rr_ps = ps.tile([P, V], F32, name="rr_ps%d" % m)
             for i, (codes, scales) in enumerate(z_q):
                 nc.tensor.matmul_mx(
                     out=rr_ps[:, i * P : (i + 1) * P],
-                    lhsT=w2_codes[:, cols].bitcast(FP8X4),
-                    lhsT_scale=w2_scales[:, cols],
+                    lhsT=w2_q[m][0][:].bitcast(FP8X4),
+                    lhsT_scale=w2_q[m][1][:],
                     rhs=codes[:].bitcast(FP8X4),
                     rhs_scale=scales[:],
                     start=True,
                     stop=True,
                 )
-            rr.append(tile([P, RR_WINDOW], F32, "rr%d" % m, "xw1" if m else None))
+            rr.append(tile([P, RR_WINDOW], F32, "rr%d" % m, None if m else "w1_raw0"))
             nc.gpsimd.memset(rr[m][:, V:], 0.0)
-            if m == 0:
-                nc.vector.tensor_scalar(rr[m][:, :V], rr_ps[:], 1.0 / D, None, ALU.mult)
-            else:
-                nc.scalar.activation(rr[m][:, :V], rr_ps[:], ACT.Copy, scale=1.0 / D)
+            nc.scalar.activation(rr[m][:, :V], rr_ps[:], ACT.Copy, scale=1.0 / D)
 
-        w3_q.append(quantized(w3_bf[1], N, "w3_1", "z1_codes"))
-        y_ps = [ps.tile([P, U], F32, name="y_ps%d" % m) for m in range(M_TILES)]
-        for g in range(PASSES):
-            for m in range(M_TILES):
+        y_ps = [ps.tile([P, U], F32, name="y_ps%d" % m, tag="y_ps1" if m else "rr_ps1") for m in range(M_TILES)]
+        for m in reversed(range(M_TILES)):
+            for g in range(PASSES):
                 cols = slice(m * P, (m + 1) * P)
                 codes, scales = w3_q[g]
                 nc.tensor.matmul_mx(
@@ -174,16 +172,23 @@ def tile_picked_ycnp_tanh_p_kernel(
                     stop=(g == PASSES - 1),
                 )
 
-        for m in range(M_TILES):
-            for r0 in range(0, U, PIECE):
-                name = "%d_%d" % (m, r0)
-                fetched = tile([P, PIECE], F32, "fetched" + name, "odd2" if (m, r0) == (1, 0) else None)
-                nc.vector.tensor_copy(fetched[:], rr[m][:].indirect(task_sb[:, r0 // 16 : (r0 + PIECE) // 16]))
-                step = PIECE // 2 if (m, r0) == (M_TILES - 1, U - PIECE) else PIECE
-                for c0 in range(0, PIECE, step):
-                    cols = slice(r0 + c0, r0 + c0 + step)
-                    summed = tile([P, step], F32, "summed%s_%d" % (name, c0))
-                    nc.vector.tensor_tensor(summed[:], fetched[:, c0 : c0 + step], y_ps[m][:, cols], ALU.add)
-                    result = tile([P, step], F32, "result%s_%d" % (name, c0))
-                    nc.scalar.activation(result[:], summed[:], ACT.Tanh)
-                    nc.sync.dma_start(out[m * P : (m + 1) * P, cols], result[:])
+        def finish(m, cols, summed):
+            result = tile([P, cols.stop - cols.start], F32, "result%d_%d" % (m, cols.start))
+            nc.scalar.activation(result[:], summed[:], ACT.Tanh)
+            nc.sync.dma_start(out[m * P : (m + 1) * P, cols], result[:])
+
+        pieces = [slice(r0, r0 + PIECE) for r0 in range(0, U, PIECE)]
+        fetched = tile([P, U], F32, "fetched")
+        for cols in pieces:
+            nc.vector.tensor_copy(fetched[:, cols], rr[0][:].indirect(task_sb[:, cols.start // 16 : cols.stop // 16]))
+        for cols in pieces:
+            y_sb = tile([P, PIECE], F32, "y_sb%d" % cols.start)
+            nc.scalar.activation(y_sb[:], y_ps[1][:, cols], ACT.Copy)
+            summed = tile([P, PIECE], F32, "summed1_%d" % cols.start)
+            window = rr[1][:].indirect(task_sb[:, cols.start // 16 : cols.stop // 16])
+            nc.vector.tensor_tensor(summed[:], window, y_sb[:], ALU.add)
+            finish(1, cols, summed)
+        for cols in (slice(0, PIECE), slice(PIECE, U - P), slice(U - P, U)):
+            summed = tile([P, cols.stop - cols.start], F32, "summed0_%d" % cols.start, None if cols.start else "y_sb0")
+            nc.vector.tensor_tensor(summed[:], fetched[:, cols], y_ps[0][:, cols], ALU.add)
+            finish(0, cols, summed)

@@ -62,6 +62,9 @@ def tile_picked_ycnp_tanh_p_kernel(
         picked_scales = tile([P, S + U], U8, "picked_scales")
         planes = tile([P, S + U], U8, "planes")
         nc.vector.memset(planes[:].bitcast(I32), 0)
+        rr = [tile([P, RR_WINDOW], F32, "rr%d" % m) for m in range(M_TILES)]
+        for m in range(M_TILES):
+            nc.vector.memset(rr[m][:, V:], 0.0)
         nc.vector.tensor_copy(picked_scales[:, :S], xs[:].indirect(offs_sb[:]))
         nc.vector.tensor_copy(picked_scales[:, S:], xs[:].indirect(tgt_sb[:]))
         for q in range(4):
@@ -77,8 +80,8 @@ def tile_picked_ycnp_tanh_p_kernel(
         for g in range(PASSES):
             ctx_words.append(gathered(xw[g], offs_sb, U32, "ctx_words%d" % g))
             tgt_words.append(gathered(xw[g], tgt_sb, U32, "tgt_words%d" % g))
-        w3_raw = [load_rows(w3, 0, "w3_raw0", "xw0")]
-        w2_raw = load_rows(w2, 0, "w2_raw", "picked_scales")
+        w2_raw = load_rows(w2, 0, "w2_raw", "xw0")
+        w3_raw = [load_rows(w3, 0, "w3_raw0", "picked_scales")]
 
         def cast(engine, dst, src):
             if engine == "scalar":
@@ -95,8 +98,8 @@ def tile_picked_ycnp_tanh_p_kernel(
         h_ps = [ps.tile([P, S], F32, name="h_ps%d" % t) for t in range(PACK)]
         for g in range(PASSES):
             src = w1_raw[g][:].rearrange("p j (m t) -> p m j t", t=PACK)
-            for u, engine in enumerate(("vector" if g else "scalar", "scalar")):
-                grouped = tile([P, 2, P, PACK], BF16, "w1_bf%d_%d" % (g, u), "w1_bf0_0" if u == 0 else None)
+            for u, engine in enumerate(("vector", "scalar") if g else ("scalar", "vector")):
+                grouped = tile([P, 2, P, PACK], BF16, "w1_bf%d_%d" % (g, u), "w1_bf0_1" if (g, u) == (1, 0) else None)
                 cast(engine, grouped[:].rearrange("p t m j -> p m j t"), src[:, :, :, 2 * u : 2 * u + 2])
                 rows = grouped[:].rearrange("p t m j -> p (t m j)")
                 codes, scales = quantized(rows, 2 * P, "w1_%d_%d" % (g, u))
@@ -122,8 +125,7 @@ def tile_picked_ycnp_tanh_p_kernel(
             return grouped[:].rearrange("p c j -> p (c j)")
 
         w3_raw.append(load_rows(w3, 1, "w3_raw1", "w1_raw0"))
-        w3_bf = [interleaved("scalar", w3_raw[0][:], "w3_bf0", "xs")]
-        w2_q = [quantized(interleaved("vector", w2_raw[:, :, :P], "w2_bf0", "w1_bf1_1"), P, "w2_0")]
+        w2_codes, w2_scales = quantized(interleaved("scalar", w2_raw[:], "w2_bf", "xs"), N, "w2")
         z_planes = tile([P, PACK, V], BF16, "z_planes")
         for t in range(PACK):
             pairs = h_ps[t][:].rearrange("p (v d) -> p d v", d=D)
@@ -136,25 +138,22 @@ def tile_picked_ycnp_tanh_p_kernel(
         z_bf = [interleaved("vector", z_planes[:, :, v0 : v0 + P], "z_bf%d" % v0) for v0 in range(0, V, P)]
         z_q = [quantized(z_bf[i], P, "z%d" % i) for i in range(V // P)]
 
-        w2_q.append(quantized(interleaved("scalar", w2_raw[:, :, P:], "w2_bf1", "odd1"), P, "w2_1", "z_bf0"))
-        w3_bf.append(interleaved("scalar", w3_raw[1][:], "w3_bf1", "odd2"))
-        w3_q = [quantized(w3_bf[0], N, "w3_0", "z_bf%d" % P), quantized(w3_bf[1], N, "w3_1", "odd1")]
-        rr = []
+        w3_bf = [interleaved("scalar", w3_raw[g][:], "w3_bf%d" % g, "odd%d" % (1 + g)) for g in range(PASSES)]
+        w3_q = [quantized(w3_bf[0], N, "w3_0", "z_bf%d" % P), quantized(w3_bf[1], N, "w3_1")]
 
         for m in range(M_TILES):
+            cols = slice(m * P, (m + 1) * P)
             rr_ps = ps.tile([P, V], F32, name="rr_ps%d" % m)
             for i, (codes, scales) in enumerate(z_q):
                 nc.tensor.matmul_mx(
                     out=rr_ps[:, i * P : (i + 1) * P],
-                    lhsT=w2_q[m][0][:].bitcast(FP8X4),
-                    lhsT_scale=w2_q[m][1][:],
+                    lhsT=w2_codes[:, cols].bitcast(FP8X4),
+                    lhsT_scale=w2_scales[:, cols],
                     rhs=codes[:].bitcast(FP8X4),
                     rhs_scale=scales[:],
                     start=True,
                     stop=True,
                 )
-            rr.append(tile([P, RR_WINDOW], F32, "rr%d" % m, None if m else "w1_raw0"))
-            nc.gpsimd.memset(rr[m][:, V:], 0.0)
             nc.scalar.activation(rr[m][:, :V], rr_ps[:], ACT.Copy, scale=1.0 / D)
 
         y_ps = [ps.tile([P, U], F32, name="y_ps%d" % m, tag="y_ps1" if m else "rr_ps1") for m in range(M_TILES)]

@@ -22,6 +22,7 @@ PASSES = K // K_PASS
 M_TILES = N // P
 RR_WINDOW = V + 32
 PIECE = 256
+SCALAR_ROWS = 88
 
 
 def tile_picked_ycnp_tanh_p_kernel(
@@ -80,8 +81,8 @@ def tile_picked_ycnp_tanh_p_kernel(
         for g in range(PASSES):
             ctx_words.append(gathered(xw[g], offs_sb, U32, "ctx_words%d" % g))
             tgt_words.append(gathered(xw[g], tgt_sb, U32, "tgt_words%d" % g))
-        w2_raw = load_rows(w2, 0, "w2_raw", "xw0")
-        w3_raw = [load_rows(w3, 0, "w3_raw0", "picked_scales")]
+        w3_raw = [load_rows(w3, 0, "w3_raw0", "xw0")]
+        w2_raw = load_rows(w2, 0, "w2_raw", "picked_scales")
 
         def cast(engine, dst, src):
             if engine == "scalar":
@@ -95,13 +96,30 @@ def tile_picked_ycnp_tanh_p_kernel(
             nc.vector.quantize_mx(out=codes[:].bitcast(FP8X4), scales=scales[:], in_=grouped)
             return codes, scales
 
+        def interleave(engine, dst, src):
+            cast(
+                engine,
+                dst.rearrange("p (c i) j -> p c j i", i=4),
+                src.rearrange("p j (c i) -> p c j i", i=4),
+            )
+
+        def flat(grouped):
+            return grouped[:].rearrange("p c j -> p (c j)")
+
         h_ps = [ps.tile([P, S], F32, name="h_ps%d" % t) for t in range(PACK)]
         for g in range(PASSES):
             src = w1_raw[g][:].rearrange("p j (m t) -> p m j t", t=PACK)
-            for u, engine in enumerate(("vector", "scalar") if g else ("scalar", "vector")):
-                grouped = tile([P, 2, P, PACK], BF16, "w1_bf%d_%d" % (g, u), "w1_bf0_1" if (g, u) == (1, 0) else None)
-                cast(engine, grouped[:].rearrange("p t m j -> p m j t"), src[:, :, :, 2 * u : 2 * u + 2])
-                rows = grouped[:].rearrange("p t m j -> p (t m j)")
+            grouped = [tile([P, 2, P, PACK], BF16, "w1_bf%d_%d" % (g, u), "w1_bf0_1" if (g, u) == (1, 0) else None) for u in range(2)]
+            dst = [t[:].rearrange("p t m j -> p m j t") for t in grouped]
+            if g == 0:
+                cast("scalar", dst[0], src[:, :, :, 0:2])
+                cast("vector", dst[1], src[:, :, :, 2:4])
+            else:
+                cast("vector", dst[0], src[:, :, :, 0:2])
+                cast("scalar", dst[1][:, :SCALAR_ROWS], src[:, :SCALAR_ROWS, :, 2:4])
+                cast("vector", dst[1][:, SCALAR_ROWS:], src[:, SCALAR_ROWS:, :, 2:4])
+            for u in range(2):
+                rows = grouped[u][:].rearrange("p t m j -> p (t m j)")
                 codes, scales = quantized(rows, 2 * P, "w1_%d_%d" % (g, u))
                 for e in range(2):
                     nc.tensor.matmul_mx(
@@ -114,18 +132,10 @@ def tile_picked_ycnp_tanh_p_kernel(
                         stop=(g == PASSES - 1),
                     )
 
-        def interleaved(engine, raw, dtype_name, tag=None):
-            width = raw.shape[2]
-            grouped = tile([P, width, PACK], BF16, dtype_name, tag)
-            cast(
-                engine,
-                grouped[:].rearrange("p (c i) j -> p c j i", i=4),
-                raw.rearrange("p j (c i) -> p c j i", i=4),
-            )
-            return grouped[:].rearrange("p c j -> p (c j)")
-
         w3_raw.append(load_rows(w3, 1, "w3_raw1", "w1_raw0"))
-        w2_codes, w2_scales = quantized(interleaved("scalar", w2_raw[:], "w2_bf", "xs"), N, "w2")
+        w3_bf = [tile([P, N, PACK], BF16, "w3_bf0")]
+        interleave("scalar", w3_bf[0][:, :P], w3_raw[0][:, :, :P])
+        interleave("vector", w3_bf[0][:, P:], w3_raw[0][:, :, P:])
         z_planes = tile([P, PACK, V], BF16, "z_planes")
         for t in range(PACK):
             pairs = h_ps[t][:].rearrange("p (v d) -> p d v", d=D)
@@ -135,20 +145,44 @@ def tile_picked_ycnp_tanh_p_kernel(
             for v0 in range(0, V, step):
                 vs = slice(v0, v0 + step)
                 nc.vector.scalar_tensor_tensor(z_planes[:, t, vs], pairs[:, 0, vs], 0.0, odd[:, vs], ALU.max, ALU.add)
-        z_bf = [interleaved("vector", z_planes[:, :, v0 : v0 + P], "z_bf%d" % v0) for v0 in range(0, V, P)]
-        z_q = [quantized(z_bf[i], P, "z%d" % i) for i in range(V // P)]
+            if t == 0:
+                w3_q = [quantized(flat(w3_bf[0]), N, "w3_0")]
+        w2_bf = [tile([P, P, PACK], BF16, "w2_bf%d" % m, "odd%d" % (1 + m)) for m in range(M_TILES)]
+        for m in range(M_TILES):
+            interleave("scalar", w2_bf[m][:], w2_raw[:, :, m * P : (m + 1) * P])
+        w2_q = [quantized(flat(w2_bf[0]), P, "w2_0")]
+        z_bf = [tile([P, P, PACK], BF16, "z_bf%d" % i) for i in range(V // P)]
+        for i in range(V // P):
+            interleave("vector", z_bf[i][:], z_planes[:, :, i * P : (i + 1) * P])
+        z_q = [quantized(flat(z_bf[i]), P, "z%d" % i) for i in range(V // P)]
 
-        w3_bf = [interleaved("scalar", w3_raw[g][:], "w3_bf%d" % g, "odd%d" % (1 + g)) for g in range(PASSES)]
-        w3_q = [quantized(w3_bf[0], N, "w3_0", "z_bf%d" % P), quantized(w3_bf[1], N, "w3_1")]
+        w2_q.append(quantized(flat(w2_bf[1]), P, "w2_1"))
+        w3_last = [tile([P, P, PACK], BF16, "w3_last%d" % m, ("odd3", "z_bf1")[m]) for m in range(M_TILES)]
+        interleave("scalar", w3_last[0][:], w3_raw[1][:, :, :P])
+        interleave("vector", w3_last[1][:], w3_raw[1][:, :, P:])
+        y_ps = [ps.tile([P, U], F32, name="y_ps%d" % m, tag="h_ps%d" % m) for m in range(M_TILES)]
+
+        def y_product(g, m, codes, scales):
+            nc.tensor.matmul_mx(
+                out=y_ps[m][:],
+                lhsT=codes.bitcast(FP8X4),
+                lhsT_scale=scales,
+                rhs=tgt_words[g][:].bitcast(FP8X4),
+                rhs_scale=planes[4 * g :, S:],
+                start=(g == 0),
+                stop=(g == PASSES - 1),
+            )
 
         for m in range(M_TILES):
-            cols = slice(m * P, (m + 1) * P)
+            y_product(0, m, w3_q[0][0][:, m * P : (m + 1) * P], w3_q[0][1][:, m * P : (m + 1) * P])
+
+        for m in range(M_TILES):
             rr_ps = ps.tile([P, V], F32, name="rr_ps%d" % m)
             for i, (codes, scales) in enumerate(z_q):
                 nc.tensor.matmul_mx(
                     out=rr_ps[:, i * P : (i + 1) * P],
-                    lhsT=w2_codes[:, cols].bitcast(FP8X4),
-                    lhsT_scale=w2_scales[:, cols],
+                    lhsT=w2_q[m][0][:].bitcast(FP8X4),
+                    lhsT_scale=w2_q[m][1][:],
                     rhs=codes[:].bitcast(FP8X4),
                     rhs_scale=scales[:],
                     start=True,
@@ -156,38 +190,33 @@ def tile_picked_ycnp_tanh_p_kernel(
                 )
             nc.scalar.activation(rr[m][:, :V], rr_ps[:], ACT.Copy, scale=1.0 / D)
 
-        y_ps = [ps.tile([P, U], F32, name="y_ps%d" % m, tag="y_ps1" if m else "rr_ps1") for m in range(M_TILES)]
-        for m in reversed(range(M_TILES)):
-            for g in range(PASSES):
-                cols = slice(m * P, (m + 1) * P)
-                codes, scales = w3_q[g]
-                nc.tensor.matmul_mx(
-                    out=y_ps[m][:],
-                    lhsT=codes[:, cols].bitcast(FP8X4),
-                    lhsT_scale=scales[:, cols],
-                    rhs=tgt_words[g][:].bitcast(FP8X4),
-                    rhs_scale=planes[4 * g :, S:],
-                    start=(g == 0),
-                    stop=(g == PASSES - 1),
-                )
+        for m in range(M_TILES):
+            codes, scales = quantized(flat(w3_last[m]), P, "w3_1_%d" % m)
+            y_product(1, m, codes[:], scales[:])
 
         def finish(m, cols, summed):
             result = tile([P, cols.stop - cols.start], F32, "result%d_%d" % (m, cols.start))
             nc.scalar.activation(result[:], summed[:], ACT.Tanh)
             nc.sync.dma_start(out[m * P : (m + 1) * P, cols], result[:])
 
-        pieces = [slice(r0, r0 + PIECE) for r0 in range(0, U, PIECE)]
-        fetched = tile([P, U], F32, "fetched")
-        for cols in pieces:
-            nc.vector.tensor_copy(fetched[:, cols], rr[0][:].indirect(task_sb[:, cols.start // 16 : cols.stop // 16]))
-        for cols in pieces:
-            y_sb = tile([P, PIECE], F32, "y_sb%d" % cols.start)
-            nc.scalar.activation(y_sb[:], y_ps[1][:, cols], ACT.Copy)
-            summed = tile([P, PIECE], F32, "summed1_%d" % cols.start)
-            window = rr[1][:].indirect(task_sb[:, cols.start // 16 : cols.stop // 16])
-            nc.vector.tensor_tensor(summed[:], window, y_sb[:], ALU.add)
-            finish(1, cols, summed)
-        for cols in (slice(0, PIECE), slice(PIECE, U - P), slice(U - P, U)):
-            summed = tile([P, cols.stop - cols.start], F32, "summed0_%d" % cols.start, None if cols.start else "y_sb0")
-            nc.vector.tensor_tensor(summed[:], fetched[:, cols], y_ps[0][:, cols], ALU.add)
-            finish(0, cols, summed)
+        def offsets(cols):
+            return task_sb[:, cols.start // 16 : cols.stop // 16]
+
+        def fused(m, cols, y_sb):
+            summed = tile([P, cols.stop - cols.start], F32, "summed%d_%d" % (m, cols.start))
+            nc.vector.tensor_tensor(summed[:], rr[m][:].indirect(offsets(cols)), y_sb, ALU.add)
+            finish(m, cols, summed)
+
+        first, second = slice(0, PIECE), slice(PIECE, U)
+        fetched = tile([P, PIECE], F32, "fetched")
+        nc.vector.tensor_copy(fetched[:], rr[0][:].indirect(offsets(first)))
+        y0_sb = tile([P, PIECE], F32, "y0_sb")
+        nc.scalar.activation(y0_sb[:], y_ps[0][:, second], ACT.Copy)
+        y1_sb = tile([P, U], F32, "y1_sb")
+        nc.scalar.activation(y1_sb[:], y_ps[1][:], ACT.Copy)
+        fused(0, second, y0_sb[:])
+        summed = tile([P, PIECE], F32, "summed0_0")
+        nc.vector.tensor_tensor(summed[:], fetched[:], y_ps[0][:, first], ALU.add)
+        finish(0, first, summed)
+        for cols in (first, slice(PIECE, U - P), slice(U - P, U)):
+            fused(1, cols, y1_sb[:, cols])

@@ -82,7 +82,7 @@ def tile_picked_ycnp_tanh_p_kernel(
             ctx_words.append(gathered(xw[g], offs_sb, U32, "ctx_words%d" % g))
             tgt_words.append(gathered(xw[g], tgt_sb, U32, "tgt_words%d" % g))
         w3_raw = [load_rows(w3, 0, "w3_raw0", "xw0")]
-        w2_raw = load_rows(w2, 0, "w2_raw", "picked_scales")
+        w3_raw.append(load_rows(w3, 1, "w3_raw1", "xw1"))
 
         def cast(engine, dst, src):
             if engine == "scalar":
@@ -113,7 +113,8 @@ def tile_picked_ycnp_tanh_p_kernel(
             dst = [t[:].rearrange("p t m j -> p m j t") for t in grouped]
             if g == 0:
                 cast("scalar", dst[0], src[:, :, :, 0:2])
-                cast("vector", dst[1], src[:, :, :, 2:4])
+                cast("vector", dst[1][:, P // 2 :], src[:, P // 2 :, :, 2:4])
+                cast("scalar", dst[1][:, : P // 2], src[:, : P // 2, :, 2:4])
             else:
                 cast("vector", dst[0], src[:, :, :, 0:2])
                 cast("scalar", dst[1][:, :SCALAR_ROWS], src[:, :SCALAR_ROWS, :, 2:4])
@@ -132,7 +133,7 @@ def tile_picked_ycnp_tanh_p_kernel(
                         stop=(g == PASSES - 1),
                     )
 
-        w3_raw.append(load_rows(w3, 1, "w3_raw1", "w1_raw0"))
+        w2_raw = load_rows(w2, 0, "w2_raw", "w1_raw0")
         w3_bf = [tile([P, N, PACK], BF16, "w3_bf0")]
         interleave("scalar", w3_bf[0][:, :P], w3_raw[0][:, :, :P])
         interleave("vector", w3_bf[0][:, P:], w3_raw[0][:, :, P:])
@@ -147,19 +148,22 @@ def tile_picked_ycnp_tanh_p_kernel(
                 nc.vector.scalar_tensor_tensor(z_planes[:, t, vs], pairs[:, 0, vs], 0.0, odd[:, vs], ALU.max, ALU.add)
             if t == 0:
                 w3_q = [quantized(flat(w3_bf[0]), N, "w3_0")]
-        w2_bf = [tile([P, P, PACK], BF16, "w2_bf%d" % m, "odd%d" % (1 + m)) for m in range(M_TILES)]
-        for m in range(M_TILES):
-            interleave("scalar", w2_bf[m][:], w2_raw[:, :, m * P : (m + 1) * P])
-        w2_q = [quantized(flat(w2_bf[0]), P, "w2_0")]
+        w2_bf = [tile([P, P, PACK], BF16, "w2_bf%d" % m, "odd%d" % (2 + m)) for m in range(M_TILES)]
+        w3_last = [tile([P, P, PACK], BF16, "w3_last0", "odd1")]
+        interleave("scalar", w3_last[0][:], w3_raw[1][:, :, :P])
+        interleave("scalar", w2_bf[0][:], w2_raw[:, :, :P])
+        interleave("scalar", w2_bf[1][:], w2_raw[:, :, P:])
+        w3_last_q = [quantized(flat(w3_last[0]), P, "w3_1_0")]
         z_bf = [tile([P, P, PACK], BF16, "z_bf%d" % i) for i in range(V // P)]
         for i in range(V // P):
             interleave("vector", z_bf[i][:], z_planes[:, :, i * P : (i + 1) * P])
+        w2_q = [quantized(flat(w2_bf[0]), P, "w2_0")]
         z_q = [quantized(flat(z_bf[i]), P, "z%d" % i) for i in range(V // P)]
 
         w2_q.append(quantized(flat(w2_bf[1]), P, "w2_1"))
-        w3_last = [tile([P, P, PACK], BF16, "w3_last%d" % m, ("odd3", "z_bf1")[m]) for m in range(M_TILES)]
-        interleave("scalar", w3_last[0][:], w3_raw[1][:, :, :P])
+        w3_last.append(tile([P, P, PACK], BF16, "w3_last1", "z_bf1"))
         interleave("vector", w3_last[1][:], w3_raw[1][:, :, P:])
+        w3_last_q.append(quantized(flat(w3_last[1]), P, "w3_1_1"))
         y_ps = [ps.tile([P, U], F32, name="y_ps%d" % m, tag="h_ps%d" % m) for m in range(M_TILES)]
 
         def y_product(g, m, codes, scales):
@@ -176,6 +180,13 @@ def tile_picked_ycnp_tanh_p_kernel(
         for m in range(M_TILES):
             y_product(0, m, w3_q[0][0][:, m * P : (m + 1) * P], w3_q[0][1][:, m * P : (m + 1) * P])
 
+        y_sb = [tile([P, PIECE], F32, "y0_first"), tile([P, U], F32, "y_sb1")]
+
+        def finish_y(m):
+            y_product(1, m, w3_last_q[m][0][:], w3_last_q[m][1][:])
+
+        finish_y(0)
+        nc.scalar.activation(y_sb[0][:], y_ps[0][:, :PIECE], ACT.Copy)
         for m in range(M_TILES):
             rr_ps = ps.tile([P, V], F32, name="rr_ps%d" % m)
             for i, (codes, scales) in enumerate(z_q):
@@ -188,11 +199,13 @@ def tile_picked_ycnp_tanh_p_kernel(
                     start=True,
                     stop=True,
                 )
+            if m:
+                finish_y(m)
             nc.scalar.activation(rr[m][:, :V], rr_ps[:], ACT.Copy, scale=1.0 / D)
-
-        for m in range(M_TILES):
-            codes, scales = quantized(flat(w3_last[m]), P, "w3_1_%d" % m)
-            y_product(1, m, codes[:], scales[:])
+            if m == 0:
+                y0_second = tile([P, PIECE], F32, "y0_second", "w2_0_codes")
+                nc.scalar.activation(y0_second[:], y_ps[0][:, PIECE:], ACT.Copy)
+        nc.scalar.activation(y_sb[1][:], y_ps[1][:], ACT.Copy)
 
         def finish(m, cols, summed):
             result = tile([P, cols.stop - cols.start], F32, "result%d_%d" % (m, cols.start))
@@ -208,15 +221,7 @@ def tile_picked_ycnp_tanh_p_kernel(
             finish(m, cols, summed)
 
         first, second = slice(0, PIECE), slice(PIECE, U)
-        fetched = tile([P, PIECE], F32, "fetched")
-        nc.vector.tensor_copy(fetched[:], rr[0][:].indirect(offsets(first)))
-        y0_sb = tile([P, PIECE], F32, "y0_sb")
-        nc.scalar.activation(y0_sb[:], y_ps[0][:, second], ACT.Copy)
-        y1_sb = tile([P, U], F32, "y1_sb")
-        nc.scalar.activation(y1_sb[:], y_ps[1][:], ACT.Copy)
-        fused(0, second, y0_sb[:])
-        summed = tile([P, PIECE], F32, "summed0_0")
-        nc.vector.tensor_tensor(summed[:], fetched[:], y_ps[0][:, first], ALU.add)
-        finish(0, first, summed)
+        fused(0, first, y_sb[0][:])
+        fused(0, second, y0_second[:])
         for cols in (first, slice(PIECE, U - P), slice(U - P, U)):
-            fused(1, cols, y1_sb[:, cols])
+            fused(1, cols, y_sb[1][:, cols])

@@ -19,10 +19,12 @@ P = 128
 PACK = 4
 K_PASS = P * PACK
 PASSES = K // K_PASS
+QUADRANTS = 4
+LIST_ROWS = 16
 M_TILES = N // P
 RR_WINDOW = V + 32
-PIECE = 256
-SCALAR_ROWS = 88
+PIECE = U // 2
+SCALAR_COLUMNS = (64, 64)
 
 
 def tile_picked_ycnp_tanh_p_kernel(
@@ -33,68 +35,24 @@ def tile_picked_ycnp_tanh_p_kernel(
         sb = ctx.enter_context(tc.tile_pool(name="sb", bufs=1))
         ps = ctx.enter_context(tc.psum_pool(name="ps", bufs=1))
 
-        def tile(shape, dtype, name, tag=None):
-            return sb.tile(shape, dtype, name=name, tag=tag or name, align_bytes=64)
+        def tile(shape, dtype, name, after=None):
+            return sb.tile(shape, dtype, name=name, tag=after or name, align_bytes=64)
 
-        offs_sb = tile([P, S // 16], U16, "offs_sb")
-        tgt_sb = tile([P, U // 16], U16, "tgt_sb")
-        task_sb = tile([P, U // 16], U16, "task_sb")
-        xs = tile([P, T], U8, "xs")
-        xw = [tile([P, T], U32, "xw%d" % g) for g in range(PASSES)]
-
-
-        def load_rows(w, g, name, tag=None):
-            raw = tile([P, PACK, w.shape[1]], F32, name, tag)
+        def load_pass(w, g, name, after=None):
+            raw = tile([P, PACK, w.shape[1]], F32, name, after)
             nc.sync.dma_start(raw[:], w[g * K_PASS : (g + 1) * K_PASS, :].rearrange("(p j) c -> p j c", j=PACK))
             return raw
 
-        for g in range(PASSES):
-            rows = x_scales[g].bitcast(I32).rearrange("(q r) c -> r q c", r=4)
-            nc.sync.dma_start(xs[16 * g : 16 * g + 16, :].bitcast(I32), rows)
-        nc.vector.memset(xs[32:64, :].bitcast(I32), 0)
-        nc.vector.memset(xs[64:, :].bitcast(I32), 0)
-        nc.sync.dma_start(offs_sb[:], offs)
-        nc.sync.dma_start(tgt_sb[:], tgt)
-        for g in range(PASSES):
-            nc.sync.dma_start(xw[g][:].bitcast(I32), x_words[g].rearrange("p c r -> p (c r)").bitcast(I32))
-        w1_raw = [load_rows(w1, 0, "w1_raw0")]
-        nc.sync.dma_start(task_sb[:], task)
-
-        picked_scales = tile([P, S + U], U8, "picked_scales")
-        planes = tile([P, S + U], U8, "planes")
-        nc.vector.memset(planes[:].bitcast(I32), 0)
-        rr = [tile([P, RR_WINDOW], F32, "rr%d" % m) for m in range(M_TILES)]
-        for m in range(M_TILES):
-            nc.vector.memset(rr[m][:, V:], 0.0)
-        nc.vector.tensor_copy(picked_scales[:, :S], xs[:].indirect(offs_sb[:]))
-        nc.vector.tensor_copy(picked_scales[:, S:], xs[:].indirect(tgt_sb[:]))
-        for q in range(4):
-            nc.sync.dma_start(planes[32 * q : 32 * q + 8, :].bitcast(I32), picked_scales[q:32:4, :].bitcast(I32))
-        w1_raw.append(load_rows(w1, 1, "w1_raw1", "xs"))
-
-        def gathered(window, offsets, dtype, name, tag=None):
-            picked = tile([P, S], dtype, name, tag)
+        def gather_words(window, offsets, name):
+            picked = tile([P, S], U32, name)
             nc.vector.tensor_copy(picked[:], window[:].indirect(offsets[:]))
             return picked
-
-        ctx_words, tgt_words = [], []
-        for g in range(PASSES):
-            ctx_words.append(gathered(xw[g], offs_sb, U32, "ctx_words%d" % g))
-            tgt_words.append(gathered(xw[g], tgt_sb, U32, "tgt_words%d" % g))
-        w3_raw = [load_rows(w3, 0, "w3_raw0", "xw0")]
-        w3_raw.append(load_rows(w3, 1, "w3_raw1", "xw1"))
 
         def cast(engine, dst, src):
             if engine == "scalar":
                 nc.scalar.activation(dst, src, ACT.Copy)
             else:
                 nc.vector.tensor_copy(dst, src)
-
-        def quantized(grouped, width, name, tag=None):
-            codes = tile([P, width], U32, name + "_codes", tag)
-            scales = tile([P, width], U8, name + "_scales")
-            nc.vector.quantize_mx(out=codes[:].bitcast(FP8X4), scales=scales[:], in_=grouped)
-            return codes, scales
 
         def interleave(engine, dst, src):
             cast(
@@ -103,125 +61,157 @@ def tile_picked_ycnp_tanh_p_kernel(
                 src.rearrange("p j (c i) -> p c j i", i=4),
             )
 
-        def flat(grouped):
-            return grouped[:].rearrange("p c j -> p (c j)")
+        def quantize(values, width, name):
+            codes = tile([P, width], U32, name + "_codes")
+            scales = tile([P, width], U8, name + "_scales")
+            nc.vector.quantize_mx(out=codes[:].bitcast(FP8X4), scales=scales[:], in_=values)
+            return codes, scales
+
+        def quantize_tile(grouped, name):
+            return quantize(grouped[:].rearrange("p c j -> p (c j)"), grouped.shape[1], name)
+
+        def product(bank, weights, cols, words, word_scales, start=True, stop=True):
+            codes, scales = weights
+            nc.tensor.matmul_mx(
+                out=bank,
+                lhsT=codes[:, cols].bitcast(FP8X4),
+                lhsT_scale=scales[:, cols],
+                rhs=words.bitcast(FP8X4),
+                rhs_scale=word_scales,
+                start=start,
+                stop=stop,
+            )
+
+        halves = [slice(0, P), slice(P, 2 * P)]
+
+        offs_sb = tile([P, S // LIST_ROWS], U16, "offs_sb")
+        tgt_sb = tile([P, U // LIST_ROWS], U16, "tgt_sb")
+        task_sb = tile([P, U // LIST_ROWS], U16, "task_sb")
+        table_scales = tile([P, T], U8, "table_scales")
+        table_words = [tile([P, T], U32, "table_words%d" % g) for g in range(PASSES)]
+
+        for g in range(PASSES):
+            rows = x_scales[g].bitcast(I32).rearrange("(q r) c -> r q c", r=4)
+            nc.sync.dma_start(table_scales[16 * g : 16 * g + 16, :].bitcast(I32), rows)
+        nc.vector.memset(table_scales[32:64, :].bitcast(I32), 0)
+        nc.vector.memset(table_scales[64:, :].bitcast(I32), 0)
+        nc.sync.dma_start(offs_sb[:], offs)
+        nc.sync.dma_start(tgt_sb[:], tgt)
+        for g in range(PASSES):
+            words = x_words[g].rearrange("p c r -> p (c r)").bitcast(I32)
+            nc.sync.dma_start(table_words[g][:].bitcast(I32), words)
+        w1_raw = [load_pass(w1, 0, "w1_raw0")]
+        nc.sync.dma_start(task_sb[:], task)
+
+        picked_scales = tile([P, S + U], U8, "picked_scales")
+        x_planes = tile([P, S + U], U8, "x_planes")
+        nc.vector.memset(x_planes[:].bitcast(I32), 0)
+        rr = [tile([P, RR_WINDOW], F32, "rr%d" % m) for m in range(M_TILES)]
+        for m in range(M_TILES):
+            nc.vector.memset(rr[m][:, V:], 0.0)
+        nc.vector.tensor_copy(picked_scales[:, :S], table_scales[:].indirect(offs_sb[:]))
+        nc.vector.tensor_copy(picked_scales[:, S:], table_scales[:].indirect(tgt_sb[:]))
+        for q in range(QUADRANTS):
+            rows = picked_scales[q:32:4, :].bitcast(I32)
+            nc.sync.dma_start(x_planes[32 * q : 32 * q + 8, :].bitcast(I32), rows)
+        w1_raw.append(load_pass(w1, 1, "w1_raw1", after="table_scales"))
+
+        ctx_words, tgt_words = [], []
+        for g in range(PASSES):
+            ctx_words.append(gather_words(table_words[g], offs_sb, "ctx_words%d" % g))
+            tgt_words.append(gather_words(table_words[g], tgt_sb, "tgt_words%d" % g))
+        w3_raw = [load_pass(w3, g, "w3_raw%d" % g, after="table_words%d" % g) for g in range(PASSES)]
 
         h_ps = [ps.tile([P, S], F32, name="h_ps%d" % t) for t in range(PACK)]
         for g in range(PASSES):
-            src = w1_raw[g][:].rearrange("p j (m t) -> p m j t", t=PACK)
-            grouped = [tile([P, 2, P, PACK], BF16, "w1_bf%d_%d" % (g, u), "w1_bf0_1" if (g, u) == (1, 0) else None) for u in range(2)]
-            dst = [t[:].rearrange("p t m j -> p m j t") for t in grouped]
-            if g == 0:
-                cast("scalar", dst[0], src[:, :, :, 0:2])
-                cast("vector", dst[1][:, P // 2 :], src[:, P // 2 :, :, 2:4])
-                cast("scalar", dst[1][:, : P // 2], src[:, : P // 2, :, 2:4])
-            else:
-                cast("vector", dst[0], src[:, :, :, 0:2])
-                cast("scalar", dst[1][:, :SCALAR_ROWS], src[:, :SCALAR_ROWS, :, 2:4])
-                cast("vector", dst[1][:, SCALAR_ROWS:], src[:, SCALAR_ROWS:, :, 2:4])
+            src = w1_raw[g][:].rearrange("p j (c t) -> p c j t", t=PACK)
+            last = g == PASSES - 1
+            pair = [
+                tile([P, 2, P, PACK], BF16, "w1_pair%d_0" % g, after="w1_pair0_1" if last else None),
+                tile([P, 2, P, PACK], BF16, "w1_pair%d_1" % g),
+            ]
+            dst = [pair[u][:].rearrange("p t c j -> p c j t") for u in range(2)]
+            share = SCALAR_COLUMNS[g]
+            cast("vector" if last else "scalar", dst[0], src[:, :, :, 0:2])
+            cast("scalar", dst[1][:, :share], src[:, :share, :, 2:4])
+            cast("vector", dst[1][:, share:], src[:, share:, :, 2:4])
             for u in range(2):
-                rows = grouped[u][:].rearrange("p t m j -> p (t m j)")
-                codes, scales = quantized(rows, 2 * P, "w1_%d_%d" % (g, u))
+                w1_q = quantize(pair[u][:].rearrange("p t c j -> p (t c j)"), 2 * P, "w1_%d_%d" % (g, u))
                 for e in range(2):
-                    nc.tensor.matmul_mx(
-                        out=h_ps[2 * u + e][:],
-                        lhsT=codes[:, e * P : (e + 1) * P].bitcast(FP8X4),
-                        lhsT_scale=scales[:, e * P : (e + 1) * P],
-                        rhs=ctx_words[g][:].bitcast(FP8X4),
-                        rhs_scale=planes[4 * g :, :S],
-                        start=(g == 0),
-                        stop=(g == PASSES - 1),
-                    )
+                    bank = h_ps[2 * u + e][:]
+                    product(bank, w1_q, halves[e], ctx_words[g][:], x_planes[4 * g :, :S], g == 0, g == PASSES - 1)
+        w2_raw = load_pass(w2, 0, "w2_raw", after="w1_raw0")
 
-        w2_raw = load_rows(w2, 0, "w2_raw", "w1_raw0")
-        w3_bf = [tile([P, N, PACK], BF16, "w3_bf0")]
-        interleave("scalar", w3_bf[0][:, :P], w3_raw[0][:, :, :P])
-        interleave("vector", w3_bf[0][:, P:], w3_raw[0][:, :, P:])
-        z_planes = tile([P, PACK, V], BF16, "z_planes")
+        w3_first = tile([P, N, PACK], BF16, "w3_first")
+        interleave("scalar", w3_first[:, halves[0]], w3_raw[0][:, :, halves[0]])
+        interleave("vector", w3_first[:, halves[1]], w3_raw[0][:, :, halves[1]])
+
+        z_rows = tile([P, PACK, V], BF16, "z_rows")
         for t in range(PACK):
-            pairs = h_ps[t][:].rearrange("p (v d) -> p d v", d=D)
+            columns = h_ps[t][:].rearrange("p (v d) -> p d v", d=D)
             odd = tile([P, V], F32, "odd%d" % t)
-            nc.scalar.activation(odd[:], pairs[:, 1], ACT.Relu)
-            step = V if t < PACK - 1 else V // 2
-            for v0 in range(0, V, step):
-                vs = slice(v0, v0 + step)
-                nc.vector.scalar_tensor_tensor(z_planes[:, t, vs], pairs[:, 0, vs], 0.0, odd[:, vs], ALU.max, ALU.add)
-            if t == 0:
-                w3_q = [quantized(flat(w3_bf[0]), N, "w3_0")]
-        w2_bf = [tile([P, P, PACK], BF16, "w2_bf%d" % m, "odd%d" % (2 + m)) for m in range(M_TILES)]
-        w3_last = [tile([P, P, PACK], BF16, "w3_last0", "odd1")]
-        interleave("scalar", w3_last[0][:], w3_raw[1][:, :, :P])
-        interleave("scalar", w2_bf[0][:], w2_raw[:, :, :P])
-        interleave("scalar", w2_bf[1][:], w2_raw[:, :, P:])
-        w3_last_q = [quantized(flat(w3_last[0]), P, "w3_1_0")]
-        z_bf = [tile([P, P, PACK], BF16, "z_bf%d" % i) for i in range(V // P)]
-        for i in range(V // P):
-            interleave("vector", z_bf[i][:], z_planes[:, :, i * P : (i + 1) * P])
-        w2_q = [quantized(flat(w2_bf[0]), P, "w2_0")]
-        z_q = [quantized(flat(z_bf[i]), P, "z%d" % i) for i in range(V // P)]
-
-        w2_q.append(quantized(flat(w2_bf[1]), P, "w2_1"))
-        w3_last.append(tile([P, P, PACK], BF16, "w3_last1", "z_bf1"))
-        interleave("vector", w3_last[1][:], w3_raw[1][:, :, P:])
-        w3_last_q.append(quantized(flat(w3_last[1]), P, "w3_1_1"))
-        y_ps = [ps.tile([P, U], F32, name="y_ps%d" % m, tag="h_ps%d" % m) for m in range(M_TILES)]
-
-        def y_product(g, m, codes, scales):
-            nc.tensor.matmul_mx(
-                out=y_ps[m][:],
-                lhsT=codes.bitcast(FP8X4),
-                lhsT_scale=scales,
-                rhs=tgt_words[g][:].bitcast(FP8X4),
-                rhs_scale=planes[4 * g :, S:],
-                start=(g == 0),
-                stop=(g == PASSES - 1),
-            )
-
-        for m in range(M_TILES):
-            y_product(0, m, w3_q[0][0][:, m * P : (m + 1) * P], w3_q[0][1][:, m * P : (m + 1) * P])
-
-        y_sb = [tile([P, PIECE], F32, "y0_first"), tile([P, U], F32, "y_sb1")]
-
-        def finish_y(m):
-            y_product(1, m, w3_last_q[m][0][:], w3_last_q[m][1][:])
-
-        finish_y(0)
-        nc.scalar.activation(y_sb[0][:], y_ps[0][:, :PIECE], ACT.Copy)
-        for m in range(M_TILES):
-            rr_ps = ps.tile([P, V], F32, name="rr_ps%d" % m)
-            for i, (codes, scales) in enumerate(z_q):
-                nc.tensor.matmul_mx(
-                    out=rr_ps[:, i * P : (i + 1) * P],
-                    lhsT=w2_q[m][0][:].bitcast(FP8X4),
-                    lhsT_scale=w2_q[m][1][:],
-                    rhs=codes[:].bitcast(FP8X4),
-                    rhs_scale=scales[:],
-                    start=True,
-                    stop=True,
+            nc.scalar.activation(odd[:], columns[:, 1], ACT.Relu)
+            for tasks in halves if t == PACK - 1 else [slice(0, V)]:
+                nc.vector.scalar_tensor_tensor(
+                    z_rows[:, t, tasks], columns[:, 0, tasks], 0.0, odd[:, tasks], ALU.max, ALU.add
                 )
-            if m:
-                finish_y(m)
-            nc.scalar.activation(rr[m][:, :V], rr_ps[:], ACT.Copy, scale=1.0 / D)
-            if m == 0:
-                y0_second = tile([P, PIECE], F32, "y0_second", "w2_0_codes")
-                nc.scalar.activation(y0_second[:], y_ps[0][:, PIECE:], ACT.Copy)
-        nc.scalar.activation(y_sb[1][:], y_ps[1][:], ACT.Copy)
+            if t == 0:
+                w3_first_q = quantize_tile(w3_first, "w3_first")
 
-        def finish(m, cols, summed):
-            result = tile([P, cols.stop - cols.start], F32, "result%d_%d" % (m, cols.start))
-            nc.scalar.activation(result[:], summed[:], ACT.Tanh)
-            nc.sync.dma_start(out[m * P : (m + 1) * P, cols], result[:])
+        w2_half = [tile([P, P, PACK], BF16, "w2_half%d" % m, after="odd%d" % (2 + m)) for m in range(M_TILES)]
+        w3_last = [tile([P, P, PACK], BF16, "w3_last0", after="odd1")]
+        interleave("scalar", w3_last[0][:], w3_raw[1][:, :, halves[0]])
+        for m in range(M_TILES):
+            interleave("scalar", w2_half[m][:], w2_raw[:, :, halves[m]])
 
-        def offsets(cols):
-            return task_sb[:, cols.start // 16 : cols.stop // 16]
+        w3_last_q = [quantize_tile(w3_last[0], "w3_last0")]
+        z_half = [tile([P, P, PACK], BF16, "z_half%d" % i) for i in range(2)]
+        for i in range(2):
+            interleave("vector", z_half[i][:], z_rows[:, :, halves[i]])
+        w2_q = [quantize_tile(w2_half[0], "w2_half0")]
+        z_q = [quantize_tile(z_half[i], "z_half%d" % i) for i in range(2)]
 
-        def fused(m, cols, y_sb):
-            summed = tile([P, cols.stop - cols.start], F32, "summed%d_%d" % (m, cols.start))
-            nc.vector.tensor_tensor(summed[:], rr[m][:].indirect(offsets(cols)), y_sb, ALU.add)
-            finish(m, cols, summed)
+        w2_q.append(quantize_tile(w2_half[1], "w2_half1"))
+        w3_last.append(tile([P, P, PACK], BF16, "w3_last1", after="z_half1"))
+        interleave("vector", w3_last[1][:], w3_raw[1][:, :, halves[1]])
+        w3_last_q.append(quantize_tile(w3_last[1], "w3_last1"))
+
+        y_ps = [ps.tile([P, U], F32, name="y_ps%d" % m, tag="h_ps%d" % m) for m in range(M_TILES)]
+        for m in range(M_TILES):
+            product(y_ps[m][:], w3_first_q, halves[m], tgt_words[0][:], x_planes[:, S:], stop=False)
+
+        def close_y(m):
+            product(y_ps[m][:], w3_last_q[m], halves[0], tgt_words[1][:], x_planes[4:, S:], start=False)
+
+        def rr_products(m):
+            for i, (z_codes, z_scales) in enumerate(z_q):
+                product(rr_ps[m][:, halves[i]], w2_q[m], halves[0], z_codes[:], z_scales[:])
 
         first, second = slice(0, PIECE), slice(PIECE, U)
-        fused(0, first, y_sb[0][:])
-        fused(0, second, y0_second[:])
+        y0_first = tile([P, PIECE], F32, "y0_first")
+        y1 = tile([P, U], F32, "y1")
+        close_y(0)
+        nc.scalar.activation(y0_first[:], y_ps[0][:, first], ACT.Copy)
+        rr_ps = [ps.tile([P, V], F32, name="rr_ps%d" % m) for m in range(M_TILES)]
+        rr_products(0)
+        nc.scalar.activation(rr[0][:, :V], rr_ps[0][:], ACT.Copy, scale=1.0 / D)
+        y0_second = tile([P, PIECE], F32, "y0_second", after="w2_half0_codes")
+        nc.scalar.activation(y0_second[:], y_ps[0][:, second], ACT.Copy)
+        rr_products(1)
+        close_y(1)
+        nc.scalar.activation(rr[1][:, :V], rr_ps[1][:], ACT.Copy, scale=1.0 / D)
+        nc.scalar.activation(y1[:], y_ps[1][:], ACT.Copy)
+
+        def finish(m, cols, y_piece):
+            width = cols.stop - cols.start
+            offsets = task_sb[:, cols.start // LIST_ROWS : cols.stop // LIST_ROWS]
+            summed = tile([P, width], F32, "summed%d_%d" % (m, cols.start))
+            nc.vector.tensor_tensor(summed[:], rr[m][:].indirect(offsets), y_piece, ALU.add)
+            result = tile([P, width], F32, "result%d_%d" % (m, cols.start))
+            nc.scalar.activation(result[:], summed[:], ACT.Tanh)
+            nc.sync.dma_start(out[halves[m], cols], result[:])
+
+        finish(0, first, y0_first[:])
+        finish(0, second, y0_second[:])
         for cols in (first, slice(PIECE, U - P), slice(U - P, U)):
-            fused(1, cols, y_sb[1][:, cols])
+            finish(1, cols, y1[:, cols])

@@ -183,23 +183,26 @@ def tile_picked_ycnp_tanh_p_kernel(
         def close_y(m):
             product(y_ps[m][:], w3_last_q[m], halves[0], tgt_words[1][:], x_planes[4:, S:], start=False)
 
-        def rr_products(m):
-            for i, (z_codes, z_scales) in enumerate(z_q):
-                product(rr_ps[m][:, halves[i]], w2_q[m], halves[0], z_codes[:], z_scales[:])
+        def rr_product(bank, m, i):
+            z_codes, z_scales = z_q[i]
+            product(bank, w2_q[m], halves[0], z_codes[:], z_scales[:])
 
         first, second = slice(0, PIECE), slice(PIECE, U)
         y0_first = tile([P, PIECE], F32, "y0_first")
         y1 = tile([P, U], F32, "y1")
         close_y(0)
         nc.scalar.activation(y0_first[:], y_ps[0][:, first], ACT.Copy)
-        rr_ps = [ps.tile([P, V], F32, name="rr_ps%d" % m) for m in range(M_TILES)]
-        rr_products(0)
-        nc.scalar.activation(rr[0][:, :V], rr_ps[0][:], ACT.Copy, scale=1.0 / D)
+        for i in range(2):
+            bank = ps.tile([P, P], F32, name="rr0_ps%d" % i)
+            rr_product(bank[:], 0, i)
+            nc.scalar.activation(rr[0][:, halves[i]], bank[:], ACT.Copy, scale=1.0 / D)
         y0_second = tile([P, PIECE], F32, "y0_second", after="w2_half0_codes")
         nc.scalar.activation(y0_second[:], y_ps[0][:, second], ACT.Copy)
-        rr_products(1)
+        bank = ps.tile([P, V], F32, name="rr1_ps")
+        for i in range(2):
+            rr_product(bank[:, halves[i]], 1, i)
         close_y(1)
-        nc.scalar.activation(rr[1][:, :V], rr_ps[1][:], ACT.Copy, scale=1.0 / D)
+        nc.scalar.activation(rr[1][:, :V], bank[:], ACT.Copy, scale=1.0 / D)
         nc.scalar.activation(y1[:], y_ps[1][:], ACT.Copy)
 
         def finish(m, cols, y_piece):

@@ -91,8 +91,7 @@ def tile_picked_ycnp_tanh_p_kernel(
         table_words = [tile([P, T], U32, "table_words%d" % g) for g in range(PASSES)]
 
         for g in range(PASSES):
-            rows = x_scales[g].bitcast(I32).rearrange("(q r) c -> r q c", r=4)
-            nc.sync.dma_start(table_scales[16 * g : 16 * g + 16, :].bitcast(I32), rows)
+            nc.sync.dma_start(table_scales[g:32:2, :].bitcast(I32), x_scales[g].bitcast(I32))
         nc.vector.memset(table_scales[32:64, :].bitcast(I32), 0)
         nc.vector.memset(table_scales[64:, :].bitcast(I32), 0)
         nc.sync.dma_start(offs_sb[:], offs)
@@ -105,15 +104,14 @@ def tile_picked_ycnp_tanh_p_kernel(
 
         picked_scales = tile([P, S + U], U8, "picked_scales")
         x_planes = tile([P, S + U], U8, "x_planes")
-        nc.vector.memset(x_planes[:].bitcast(I32), 0)
         rr = [tile([P, RR_WINDOW], F32, "rr%d" % m) for m in range(M_TILES)]
         for m in range(M_TILES):
             nc.vector.memset(rr[m][:, V:], 0.0)
         nc.vector.tensor_copy(picked_scales[:, :S], table_scales[:].indirect(offs_sb[:]))
         nc.vector.tensor_copy(picked_scales[:, S:], table_scales[:].indirect(tgt_sb[:]))
-        for q in range(QUADRANTS):
-            rows = picked_scales[q:32:4, :].bitcast(I32)
-            nc.sync.dma_start(x_planes[32 * q : 32 * q + 8, :].bitcast(I32), rows)
+        for r in range(4):
+            rows = picked_scales[2 * r : 2 * r + 32, :].bitcast(I32)
+            nc.sync.dma_start(x_planes[r::4, :].bitcast(I32), rows)
         w1_raw.append(load_pass(w1, 1, "w1_raw1", after="table_scales"))
 
         ctx_words, tgt_words = [], []

@@ -61,14 +61,14 @@ def tile_picked_ycnp_tanh_p_kernel(
                 src.rearrange("p j (c i) -> p c j i", i=4),
             )
 
-        def quantize(values, width, name):
-            codes = tile([P, width], U32, name + "_codes")
+        def quantize(values, width, name, after=None):
+            codes = tile([P, width], U32, name + "_codes", after)
             scales = tile([P, width], U8, name + "_scales")
             nc.vector.quantize_mx(out=codes[:].bitcast(FP8X4), scales=scales[:], in_=values)
             return codes, scales
 
-        def quantize_tile(grouped, name):
-            return quantize(grouped[:].rearrange("p c j -> p (c j)"), grouped.shape[1], name)
+        def quantize_tile(grouped, name, after=None):
+            return quantize(grouped[:].rearrange("p c j -> p (c j)"), grouped.shape[1], name, after)
 
         def product(bank, weights, cols, words, word_scales, start=True, stop=True):
             codes, scales = weights
@@ -90,8 +90,7 @@ def tile_picked_ycnp_tanh_p_kernel(
         table_scales = tile([P, T], U8, "table_scales")
         table_words = [tile([P, T], U32, "table_words%d" % g) for g in range(PASSES)]
 
-        for g in range(PASSES):
-            nc.sync.dma_start(table_scales[g:32:2, :].bitcast(I32), x_scales[g].bitcast(I32))
+        nc.sync.dma_start(table_scales[:32, :].bitcast(I32), x_scales.bitcast(I32).rearrange("g j c -> j g c"))
         nc.vector.memset(table_scales[32:64, :].bitcast(I32), 0)
         nc.vector.memset(table_scales[64:, :].bitcast(I32), 0)
         nc.sync.dma_start(offs_sb[:], offs)
@@ -120,7 +119,7 @@ def tile_picked_ycnp_tanh_p_kernel(
             tgt_words.append(gather_words(table_words[g], tgt_sb, "tgt_words%d" % g))
         w3_raw = [load_pass(w3, g, "w3_raw%d" % g, after="table_words%d" % g) for g in range(PASSES)]
 
-        h_ps = [ps.tile([P, S], F32, name="h_ps%d" % t) for t in range(PACK)]
+        h_ps = [ps.tile([P, 2, S // 2], F32, name="h_ps%d" % b) for b in range(4)]
         for g in range(PASSES):
             src = w1_raw[g][:].rearrange("p j (c t) -> p c j t", t=PACK)
             last = g == PASSES - 1
@@ -135,48 +134,21 @@ def tile_picked_ycnp_tanh_p_kernel(
             cast("vector", dst[1][:, share:], src[:, share:, :, 2:4])
             for u in range(2):
                 w1_q = quantize(pair[u][:].rearrange("p t c j -> p (t c j)"), 2 * P, "w1_%d_%d" % (g, u))
-                for e in range(2):
-                    bank = h_ps[2 * u + e][:]
-                    product(bank, w1_q, halves[e], ctx_words[g][:], x_planes[4 * g :, :S], g == 0, g == PASSES - 1)
+                for i in range(2):
+                    entries = slice(i * S // 2, (i + 1) * S // 2)
+                    for e in range(2):
+                        product(
+                            h_ps[2 * u + i][:, e],
+                            w1_q,
+                            halves[e],
+                            ctx_words[g][:, entries],
+                            x_planes[4 * g :, entries],
+                            start=g == 0 and e == 0,
+                            stop=last and e == 1,
+                        )
         w2_raw = load_pass(w2, 0, "w2_raw", after="w1_raw0")
 
-        w3_first = tile([P, N, PACK], BF16, "w3_first")
-        interleave("scalar", w3_first[:, halves[0]], w3_raw[0][:, :, halves[0]])
-        interleave("vector", w3_first[:, halves[1]], w3_raw[0][:, :, halves[1]])
-
-        z_rows = tile([P, PACK, V], BF16, "z_rows")
-        for t in range(PACK):
-            columns = h_ps[t][:].rearrange("p (v d) -> p d v", d=D)
-            odd = tile([P, V], F32, "odd%d" % t)
-            nc.scalar.activation(odd[:], columns[:, 1], ACT.Relu)
-            for tasks in halves if t == PACK - 1 else [slice(0, V)]:
-                nc.vector.scalar_tensor_tensor(
-                    z_rows[:, t, tasks], columns[:, 0, tasks], 0.0, odd[:, tasks], ALU.max, ALU.add
-                )
-            if t == 0:
-                w3_first_q = quantize_tile(w3_first, "w3_first")
-
-        w2_half = [tile([P, P, PACK], BF16, "w2_half%d" % m, after="odd%d" % (2 + m)) for m in range(M_TILES)]
-        w3_last = [tile([P, P, PACK], BF16, "w3_last0", after="odd1")]
-        interleave("scalar", w3_last[0][:], w3_raw[1][:, :, halves[0]])
-        for m in range(M_TILES):
-            interleave("scalar", w2_half[m][:], w2_raw[:, :, halves[m]])
-
-        w3_last_q = [quantize_tile(w3_last[0], "w3_last0")]
-        z_half = [tile([P, P, PACK], BF16, "z_half%d" % i) for i in range(2)]
-        for i in range(2):
-            interleave("vector", z_half[i][:], z_rows[:, :, halves[i]])
-        w2_q = [quantize_tile(w2_half[0], "w2_half0")]
-        z_q = [quantize_tile(z_half[i], "z_half%d" % i) for i in range(2)]
-
-        w2_q.append(quantize_tile(w2_half[1], "w2_half1"))
-        w3_last.append(tile([P, P, PACK], BF16, "w3_last1", after="z_half1"))
-        interleave("vector", w3_last[1][:], w3_raw[1][:, :, halves[1]])
-        w3_last_q.append(quantize_tile(w3_last[1], "w3_last1"))
-
-        y_ps = [ps.tile([P, U], F32, name="y_ps%d" % m, tag="h_ps%d" % m) for m in range(M_TILES)]
-        for m in range(M_TILES):
-            product(y_ps[m][:], w3_first_q, halves[m], tgt_words[0][:], x_planes[:, S:], stop=False)
+        y_ps = [ps.tile([P, U], F32, name="y_ps%d" % m) for m in range(M_TILES)]
 
         def close_y(m):
             product(y_ps[m][:], w3_last_q[m], halves[0], tgt_words[1][:], x_planes[4:, S:], start=False)
@@ -185,34 +157,78 @@ def tile_picked_ycnp_tanh_p_kernel(
             z_codes, z_scales = z_q[i]
             product(bank, w2_q[m], halves[0], z_codes[:], z_scales[:])
 
+        w3_first = [tile([P, P, PACK], BF16, "w3_first%d" % m) for m in range(M_TILES)]
+        for m in range(M_TILES):
+            interleave("scalar", w3_first[m][:], w3_raw[0][:, :, halves[m]])
+        for m in range(M_TILES):
+            w3_first_q = quantize_tile(w3_first[m], "w3_first%d" % m)
+            product(y_ps[m][:], w3_first_q, halves[0], tgt_words[0][:], x_planes[:, S:], stop=False)
+        w3_last = [tile([P, P, PACK], BF16, "w3_last0", after="w3_first0")]
+        interleave("vector", w3_last[0][:], w3_raw[1][:, :, halves[0]])
+
+        z_pairs = [tile([P, 2, P, 2], BF16, "z_pairs%d" % i) for i in range(2)]
+        z_half = [tile([P, P, PACK], BF16, "z_half%d" % i) for i in range(2)]
+
+        def weave(i):
+            dst = z_half[i][:].rearrange("p c j -> p (c j)").bitcast(I32).rearrange("p (c n u) -> p c u n", n=2, u=2)
+            src = z_pairs[i][:].rearrange("p u c e -> p (u c e)").bitcast(I32)
+            nc.vector.tensor_copy(dst, src.rearrange("p (u c n) -> p c u n", u=2, n=2))
+
+        for b in range(4):
+            u, i = divmod(b, 2)
+            columns = h_ps[b][:].rearrange("p e (v d) -> p d v e", d=D)
+            odd = tile([P, P, 2], F32, "odd%d" % b, after="table_words0" if b == 0 else None)
+            nc.scalar.activation(odd[:], columns[:, 1], ACT.Relu)
+            nc.vector.scalar_tensor_tensor(z_pairs[i][:, u], columns[:, 0], 0.0, odd[:], ALU.max, ALU.add)
+            if b == 0:
+                w3_last_q = [quantize_tile(w3_last[0], "w3_last0")]
+                close_y(0)
+
         first, second = slice(0, PIECE), slice(PIECE, U)
-        y0_first = tile([P, PIECE], F32, "y0_first")
-        y1 = tile([P, U], F32, "y1")
-        close_y(0)
+        w2_half = [
+            tile([P, P, PACK], BF16, "w2_half0", after="table_words0"),
+            tile([P, P, PACK], BF16, "w2_half1", after="odd2"),
+        ]
+        interleave("scalar", w2_half[0][:], w2_raw[:, :, halves[0]])
+        y0_first = tile([P, PIECE], F32, "y0_first", after="odd1")
         nc.scalar.activation(y0_first[:], y_ps[0][:, first], ACT.Copy)
+        interleave("scalar", w2_half[1][:], w2_raw[:, :, halves[1]])
+
+        weave(0)
+        weave(1)
+        z_q = [quantize_tile(z_half[0], "z_half0")]
+        w2_q = [quantize_tile(w2_half[0], "w2_half0")]
+        z_q.append(quantize_tile(z_half[1], "z_half1"))
+        w3_last.append(tile([P, P, PACK], BF16, "w3_last1", after="table_words0"))
+        interleave("vector", w3_last[1][:], w3_raw[1][:, :, halves[1]])
+        w2_q.append(quantize_tile(w2_half[1], "w2_half1"))
+        w3_last_q.append(quantize_tile(w3_last[1], "w3_last1"))
+
+        y1 = tile([P, U], F32, "y1")
         for i in range(2):
             bank = ps.tile([P, P], F32, name="rr0_ps%d" % i)
             rr_product(bank[:], 0, i)
             nc.scalar.activation(rr[0][:, halves[i]], bank[:], ACT.Copy, scale=1.0 / D)
         y0_second = tile([P, PIECE], F32, "y0_second", after="w2_half0_codes")
         nc.scalar.activation(y0_second[:], y_ps[0][:, second], ACT.Copy)
-        bank = ps.tile([P, V], F32, name="rr1_ps")
+        bank = ps.tile([P, V], F32, name="rr1_ps", tag="h_ps0")
         for i in range(2):
             rr_product(bank[:, halves[i]], 1, i)
         close_y(1)
         nc.scalar.activation(rr[1][:, :V], bank[:], ACT.Copy, scale=1.0 / D)
-        nc.scalar.activation(y1[:], y_ps[1][:], ACT.Copy)
+        nc.scalar.activation(y1[:, first], y_ps[1][:, first], ACT.Copy)
 
-        def finish(m, cols, y_piece):
+        def finish(m, cols, y_piece, after=None, after_tanh=None):
             width = cols.stop - cols.start
             offsets = task_sb[:, cols.start // LIST_ROWS : cols.stop // LIST_ROWS]
-            summed = tile([P, width], F32, "summed%d_%d" % (m, cols.start))
+            summed = tile([P, width], F32, "summed%d_%d" % (m, cols.start), after)
             nc.vector.tensor_tensor(summed[:], rr[m][:].indirect(offsets), y_piece, ALU.add)
-            result = tile([P, width], F32, "result%d_%d" % (m, cols.start))
+            result = tile([P, width], F32, "result%d_%d" % (m, cols.start), after_tanh)
             nc.scalar.activation(result[:], summed[:], ACT.Tanh)
             nc.sync.dma_start(out[halves[m], cols], result[:])
 
-        finish(0, first, y0_first[:])
+        finish(0, first, y0_first[:], after="odd2", after_tanh="w3_last1_codes")
+        nc.scalar.activation(y1[:, second], y_ps[1][:, second], ACT.Copy)
         finish(0, second, y0_second[:])
         for cols in (first, slice(PIECE, U - P), slice(U - P, U)):
             finish(1, cols, y1[:, cols])

@@ -33,9 +33,12 @@ def tile_picked_ycnp_tanh_p_kernel(
     nc = tc.nc
     with ExitStack() as ctx:
         sb = ctx.enter_context(tc.tile_pool(name="sb", bufs=1))
+        shared = ctx.enter_context(tc.tile_pool(name="shared", bufs=1))
         ps = ctx.enter_context(tc.psum_pool(name="ps", bufs=1))
 
         def tile(shape, dtype, name, after=None):
+            if isinstance(after, int):
+                return shared.tile(shape, dtype, name=name, offset=after * 1024, align_bytes=64)
             return sb.tile(shape, dtype, name=name, tag=after or name, align_bytes=64)
 
         def load_pass(w, g, name, after=None):
@@ -88,11 +91,10 @@ def tile_picked_ycnp_tanh_p_kernel(
         tgt_sb = tile([P, U // LIST_ROWS], U16, "tgt_sb")
         task_sb = tile([P, U // LIST_ROWS], U16, "task_sb")
         table_scales = tile([P, T], U8, "table_scales")
-        table_words = [tile([P, T], U32, "table_words%d" % g) for g in range(PASSES)]
+        table_words = [tile([P, T], U32, "table_words0", after=0), tile([P, T], U32, "table_words1")]
 
-        nc.sync.dma_start(table_scales[:32, :].bitcast(I32), x_scales.bitcast(I32).rearrange("g j c -> j g c"))
-        nc.vector.memset(table_scales[32:64, :].bitcast(I32), 0)
-        nc.vector.memset(table_scales[64:, :].bitcast(I32), 0)
+        nc.sync.dma_start(table_scales[96:, :].bitcast(I32), x_scales.bitcast(I32).rearrange("g j c -> (g j) c"))
+        nc.vector.memset(table_scales[:96, :].bitcast(I32), 0)
         nc.sync.dma_start(offs_sb[:], offs)
         nc.sync.dma_start(tgt_sb[:], tgt)
         for g in range(PASSES):
@@ -102,22 +104,30 @@ def tile_picked_ycnp_tanh_p_kernel(
         nc.sync.dma_start(task_sb[:], task)
 
         picked_scales = tile([P, S + U], U8, "picked_scales")
-        x_planes = tile([P, S + U], U8, "x_planes")
+        x_planes = [tile([P, S + U], U8, "x_planes%d" % g) for g in range(PASSES)]
+        for g in range(PASSES):
+            nc.vector.memset(x_planes[g][:].bitcast(I32), 0)
         rr = [tile([P, RR_WINDOW], F32, "rr%d" % m) for m in range(M_TILES)]
         for m in range(M_TILES):
             nc.vector.memset(rr[m][:, V:], 0.0)
         nc.vector.tensor_copy(picked_scales[:, :S], table_scales[:].indirect(offs_sb[:]))
         nc.vector.tensor_copy(picked_scales[:, S:], table_scales[:].indirect(tgt_sb[:]))
-        for r in range(4):
-            rows = picked_scales[2 * r : 2 * r + 32, :].bitcast(I32)
-            nc.sync.dma_start(x_planes[r::4, :].bitcast(I32), rows)
+
+        def move_scales(g):
+            for q in range(QUADRANTS):
+                row = 96 + 16 * g + 4 * q
+                rows = picked_scales[row : row + 4, :].bitcast(I32)
+                nc.sync.dma_start(x_planes[g][32 * q : 32 * q + 4, :].bitcast(I32), rows)
+
+        move_scales(0)
         w1_raw.append(load_pass(w1, 1, "w1_raw1", after="table_scales"))
+        move_scales(1)
 
         ctx_words, tgt_words = [], []
         for g in range(PASSES):
             ctx_words.append(gather_words(table_words[g], offs_sb, "ctx_words%d" % g))
             tgt_words.append(gather_words(table_words[g], tgt_sb, "tgt_words%d" % g))
-        w3_raw = [load_pass(w3, g, "w3_raw%d" % g, after="table_words%d" % g) for g in range(PASSES)]
+        w3_raw = [load_pass(w3, g, "w3_raw%d" % g, after=(0, "table_words1")[g]) for g in range(PASSES)]
 
         h_ps = [ps.tile([P, 2, S // 2], F32, name="h_ps%d" % b) for b in range(4)]
         for g in range(PASSES):
@@ -142,7 +152,7 @@ def tile_picked_ycnp_tanh_p_kernel(
                             w1_q,
                             halves[e],
                             ctx_words[g][:, entries],
-                            x_planes[4 * g :, entries],
+                            x_planes[g][:, entries],
                             start=g == 0 and e == 0,
                             stop=last and e == 1,
                         )
@@ -151,7 +161,7 @@ def tile_picked_ycnp_tanh_p_kernel(
         y_ps = [ps.tile([P, U], F32, name="y_ps%d" % m) for m in range(M_TILES)]
 
         def close_y(m):
-            product(y_ps[m][:], w3_last_q[m], halves[0], tgt_words[1][:], x_planes[4:, S:], start=False)
+            product(y_ps[m][:], w3_last_q[m], halves[0], tgt_words[1][:], x_planes[1][:, S:], start=False)
 
         def rr_product(bank, m, i):
             z_codes, z_scales = z_q[i]
@@ -162,7 +172,7 @@ def tile_picked_ycnp_tanh_p_kernel(
             interleave("scalar", w3_first[m][:], w3_raw[0][:, :, halves[m]])
         for m in range(M_TILES):
             w3_first_q = quantize_tile(w3_first[m], "w3_first%d" % m)
-            product(y_ps[m][:], w3_first_q, halves[0], tgt_words[0][:], x_planes[:, S:], stop=False)
+            product(y_ps[m][:], w3_first_q, halves[0], tgt_words[0][:], x_planes[0][:, S:], stop=False)
         w3_last = [tile([P, P, PACK], BF16, "w3_last0", after="w3_first0")]
         interleave("vector", w3_last[0][:], w3_raw[1][:, :, halves[0]])
 
@@ -177,7 +187,7 @@ def tile_picked_ycnp_tanh_p_kernel(
         for b in range(4):
             u, i = divmod(b, 2)
             columns = h_ps[b][:].rearrange("p e (v d) -> p d v e", d=D)
-            odd = tile([P, P, 2], F32, "odd%d" % b, after="table_words0" if b == 0 else None)
+            odd = tile([P, P, 2], F32, "odd%d" % b, after=b)
             nc.scalar.activation(odd[:], columns[:, 1], ACT.Relu)
             nc.vector.scalar_tensor_tensor(z_pairs[i][:, u], columns[:, 0], 0.0, odd[:], ALU.max, ALU.add)
             if b == 0:
@@ -186,11 +196,11 @@ def tile_picked_ycnp_tanh_p_kernel(
 
         first, second = slice(0, PIECE), slice(PIECE, U)
         w2_half = [
-            tile([P, P, PACK], BF16, "w2_half0", after="table_words0"),
-            tile([P, P, PACK], BF16, "w2_half1", after="odd2"),
+            tile([P, P, PACK], BF16, "w2_half0", after=0),
+            tile([P, P, PACK], BF16, "w2_half1", after=2),
         ]
         interleave("scalar", w2_half[0][:], w2_raw[:, :, halves[0]])
-        y0_first = tile([P, PIECE], F32, "y0_first", after="odd1")
+        y0_first = tile([P, PIECE], F32, "y0_first", after=1)
         nc.scalar.activation(y0_first[:], y_ps[0][:, first], ACT.Copy)
         interleave("scalar", w2_half[1][:], w2_raw[:, :, halves[1]])
 
@@ -199,7 +209,7 @@ def tile_picked_ycnp_tanh_p_kernel(
         z_q = [quantize_tile(z_half[0], "z_half0")]
         w2_q = [quantize_tile(w2_half[0], "w2_half0")]
         z_q.append(quantize_tile(z_half[1], "z_half1"))
-        w3_last.append(tile([P, P, PACK], BF16, "w3_last1", after="table_words0"))
+        w3_last.append(tile([P, P, PACK], BF16, "w3_last1", after=0))
         interleave("vector", w3_last[1][:], w3_raw[1][:, :, halves[1]])
         w2_q.append(quantize_tile(w2_half[1], "w2_half1"))
         w3_last_q.append(quantize_tile(w3_last[1], "w3_last1"))
@@ -227,7 +237,7 @@ def tile_picked_ycnp_tanh_p_kernel(
             nc.scalar.activation(result[:], summed[:], ACT.Tanh)
             nc.sync.dma_start(out[halves[m], cols], result[:])
 
-        finish(0, first, y0_first[:], after="odd2", after_tanh="w3_last1_codes")
+        finish(0, first, y0_first[:], after=2, after_tanh="w3_last1_codes")
         nc.scalar.activation(y1[:, second], y_ps[1][:, second], ACT.Copy)
         finish(0, second, y0_second[:])
         for cols in (first, slice(PIECE, U - P), slice(U - P, U)):

@@ -158,10 +158,20 @@ def tile_picked_ycnp_tanh_p_kernel(
                         )
         w2_raw = load_pass(w2, 0, "w2_raw", after="w1_raw0")
 
-        y_ps = [ps.tile([P, U], F32, name="y_ps%d" % m) for m in range(M_TILES)]
+        first, second = slice(0, PIECE), slice(PIECE, U)
+        y_pieces = [[slice(0, U)], [first, second]]
+        y_ps = [
+            [ps.tile([P, cols.stop - cols.start], F32, name="y_ps%d_%d" % (m, cols.start)) for cols in y_pieces[m]]
+            for m in range(M_TILES)
+        ]
+
+        def y_pass(g, m, weights):
+            for bank, cols in zip(y_ps[m], y_pieces[m]):
+                planes = x_planes[g][:, S + cols.start : S + cols.stop]
+                product(bank[:], weights, halves[0], tgt_words[g][:, cols], planes, start=g == 0, stop=g == 1)
 
         def close_y(m):
-            product(y_ps[m][:], w3_last_q[m], halves[0], tgt_words[1][:], x_planes[1][:, S:], start=False)
+            y_pass(1, m, w3_last_q[m])
 
         def rr_product(bank, m, i):
             z_codes, z_scales = z_q[i]
@@ -172,7 +182,7 @@ def tile_picked_ycnp_tanh_p_kernel(
             interleave("scalar", w3_first[m][:], w3_raw[0][:, :, halves[m]])
         for m in range(M_TILES):
             w3_first_q = quantize_tile(w3_first[m], "w3_first%d" % m)
-            product(y_ps[m][:], w3_first_q, halves[0], tgt_words[0][:], x_planes[0][:, S:], stop=False)
+            y_pass(0, m, w3_first_q)
         w3_last = [tile([P, P, PACK], BF16, "w3_last0", after="w3_first0")]
         interleave("vector", w3_last[0][:], w3_raw[1][:, :, halves[0]])
 
@@ -194,14 +204,13 @@ def tile_picked_ycnp_tanh_p_kernel(
                 w3_last_q = [quantize_tile(w3_last[0], "w3_last0")]
                 close_y(0)
 
-        first, second = slice(0, PIECE), slice(PIECE, U)
         w2_half = [
             tile([P, P, PACK], BF16, "w2_half0", after=0),
             tile([P, P, PACK], BF16, "w2_half1", after=2),
         ]
         interleave("scalar", w2_half[0][:], w2_raw[:, :, halves[0]])
         y0_first = tile([P, PIECE], F32, "y0_first", after=1)
-        nc.scalar.activation(y0_first[:], y_ps[0][:, first], ACT.Copy)
+        nc.scalar.activation(y0_first[:], y_ps[0][0][:, first], ACT.Copy)
         interleave("scalar", w2_half[1][:], w2_raw[:, :, halves[1]])
 
         weave(0)
@@ -216,17 +225,17 @@ def tile_picked_ycnp_tanh_p_kernel(
 
         y1 = tile([P, U], F32, "y1")
         for i in range(2):
-            bank = ps.tile([P, P], F32, name="rr0_ps%d" % i)
+            bank = ps.tile([P, P], F32, name="rr0_ps%d" % i, tag="h_ps%d" % (i + 1))
             rr_product(bank[:], 0, i)
             nc.scalar.activation(rr[0][:, halves[i]], bank[:], ACT.Copy, scale=1.0 / D)
         y0_second = tile([P, PIECE], F32, "y0_second", after="w2_half0_codes")
-        nc.scalar.activation(y0_second[:], y_ps[0][:, second], ACT.Copy)
+        nc.scalar.activation(y0_second[:], y_ps[0][0][:, second], ACT.Copy)
         bank = ps.tile([P, V], F32, name="rr1_ps", tag="h_ps0")
         for i in range(2):
             rr_product(bank[:, halves[i]], 1, i)
         close_y(1)
         nc.scalar.activation(rr[1][:, :V], bank[:], ACT.Copy, scale=1.0 / D)
-        nc.scalar.activation(y1[:, first], y_ps[1][:, first], ACT.Copy)
+        nc.scalar.activation(y1[:, first], y_ps[1][0][:], ACT.Copy)
 
         def finish(m, cols, y_piece, after=None, after_tanh=None):
             width = cols.stop - cols.start
@@ -238,7 +247,7 @@ def tile_picked_ycnp_tanh_p_kernel(
             nc.sync.dma_start(out[halves[m], cols], result[:])
 
         finish(0, first, y0_first[:], after=2, after_tanh="w3_last1_codes")
-        nc.scalar.activation(y1[:, second], y_ps[1][:, second], ACT.Copy)
+        nc.scalar.activation(y1[:, second], y_ps[1][1][:], ACT.Copy)
         finish(0, second, y0_second[:])
         for cols in (first, slice(PIECE, U - P), slice(U - P, U)):
             finish(1, cols, y1[:, cols])

@@ -24,7 +24,7 @@ LIST_ROWS = 16
 M_TILES = N // P
 RR_WINDOW = V + 32
 PIECE = U // 2
-SCALAR_COLUMNS = (64, 64)
+SCALAR_COLUMNS = (48, 64)
 
 
 def tile_picked_ycnp_tanh_p_kernel(
@@ -54,6 +54,8 @@ def tile_picked_ycnp_tanh_p_kernel(
         def cast(engine, dst, src):
             if engine == "scalar":
                 nc.scalar.activation(dst, src, ACT.Copy)
+            elif engine == "gpsimd":
+                nc.gpsimd.tensor_scalar(dst, src, 1.0, 0.0, ALU.mult, ALU.add)
             else:
                 nc.vector.tensor_copy(dst, src)
 
@@ -141,7 +143,11 @@ def tile_picked_ycnp_tanh_p_kernel(
             share = SCALAR_COLUMNS[g]
             cast("vector" if last else "scalar", dst[0], src[:, :, :, 0:2])
             cast("scalar", dst[1][:, :share], src[:, :share, :, 2:4])
-            cast("vector", dst[1][:, share:], src[:, share:, :, 2:4])
+            if last:
+                cast("vector", dst[1][:, share:], src[:, share:, :, 2:4])
+            else:
+                for e in range(2):
+                    cast("gpsimd", pair[1][:, e, share:], src[:, share:, :, 2 + e])
             for u in range(2):
                 w1_q = quantize(pair[u][:].rearrange("p t c j -> p (t c j)"), 2 * P, "w1_%d_%d" % (g, u))
                 for i in range(2):

@@ -103,7 +103,6 @@ def tile_picked_ycnp_tanh_p_kernel(
             words = x_words[g].rearrange("p c r -> p (c r)").bitcast(I32)
             nc.sync.dma_start(table_words[g][:].bitcast(I32), words)
         w1_raw = [load_pass(w1, 0, "w1_raw0")]
-        nc.sync.dma_start(task_sb[:], task)
 
         picked_scales = tile([P, S + U], U8, "picked_scales")
         x_planes = [tile([P, S + U], U8, "x_planes%d" % g) for g in range(PASSES)]
@@ -119,7 +118,7 @@ def tile_picked_ycnp_tanh_p_kernel(
             for q in range(QUADRANTS):
                 row = 96 + 16 * g + 4 * q
                 rows = picked_scales[row : row + 4, :].bitcast(I32)
-                nc.sync.dma_start(x_planes[g][32 * q : 32 * q + 4, :].bitcast(I32), rows)
+                nc.sync.dma_start(x_planes[g][32 * q + 4 * g : 32 * q + 4 * g + 4, :].bitcast(I32), rows)
 
         move_scales(0)
         w1_raw.append(load_pass(w1, 1, "w1_raw1", after="table_scales"))
@@ -158,11 +157,12 @@ def tile_picked_ycnp_tanh_p_kernel(
                             w1_q,
                             halves[e],
                             ctx_words[g][:, entries],
-                            x_planes[g][:, entries],
+                            x_planes[g][4 * g :, entries],
                             start=g == 0 and e == 0,
                             stop=last and e == 1,
                         )
         w2_raw = load_pass(w2, 0, "w2_raw", after="w1_raw0")
+        nc.sync.dma_start(task_sb[:], task)
 
         first, second = slice(0, PIECE), slice(PIECE, U)
         y_pieces = [[slice(0, U)], [first, second]]
@@ -173,7 +173,7 @@ def tile_picked_ycnp_tanh_p_kernel(
 
         def y_pass(g, m, weights):
             for bank, cols in zip(y_ps[m], y_pieces[m]):
-                planes = x_planes[g][:, S + cols.start : S + cols.stop]
+                planes = x_planes[g][4 * g :, S + cols.start : S + cols.stop]
                 product(bank[:], weights, halves[0], tgt_words[g][:, cols], planes, start=g == 0, stop=g == 1)
 
         def close_y(m):

@@ -24,7 +24,7 @@ LIST_ROWS = 16
 M_TILES = N // P
 RR_WINDOW = V + 32
 PIECE = U // 2
-SCALAR_COLUMNS = (48, 64)
+SCALAR_COLUMNS = ((96, 48), (0, 64))
 
 
 def tile_picked_ycnp_tanh_p_kernel(
@@ -54,8 +54,6 @@ def tile_picked_ycnp_tanh_p_kernel(
         def cast(engine, dst, src):
             if engine == "scalar":
                 nc.scalar.activation(dst, src, ACT.Copy)
-            elif engine == "gpsimd":
-                nc.gpsimd.tensor_scalar(dst, src, 1.0, 0.0, ALU.mult, ALU.add)
             else:
                 nc.vector.tensor_copy(dst, src)
 
@@ -139,14 +137,11 @@ def tile_picked_ycnp_tanh_p_kernel(
                 tile([P, 2, P, PACK], BF16, "w1_pair%d_1" % g),
             ]
             dst = [pair[u][:].rearrange("p t c j -> p c j t") for u in range(2)]
-            share = SCALAR_COLUMNS[g]
-            cast("vector" if last else "scalar", dst[0], src[:, :, :, 0:2])
-            cast("scalar", dst[1][:, :share], src[:, :share, :, 2:4])
-            if last:
-                cast("vector", dst[1][:, share:], src[:, share:, :, 2:4])
-            else:
-                for e in range(2):
-                    cast("gpsimd", pair[1][:, e, share:], src[:, share:, :, 2 + e])
+            for u in range(2):
+                share = SCALAR_COLUMNS[g][u]
+                if share:
+                    cast("scalar", dst[u][:, :share], src[:, :share, :, 2 * u : 2 * u + 2])
+                cast("vector", dst[u][:, share:], src[:, share:, :, 2 * u : 2 * u + 2])
             for u in range(2):
                 w1_q = quantize(pair[u][:].rearrange("p t c j -> p (t c j)"), 2 * P, "w1_%d_%d" % (g, u))
                 for i in range(2):

@@ -24,7 +24,7 @@ LIST_ROWS = 16
 M_TILES = N // P
 RR_WINDOW = V + 32
 PIECE = U // 2
-SCALAR_COLUMNS = ((96, 48), (0, 64))
+SCALAR_COLUMNS = ((64, 48), (0, 64))
 
 
 def tile_picked_ycnp_tanh_p_kernel(

@@ -24,7 +24,7 @@ LIST_ROWS = 16
 M_TILES = N // P
 RR_WINDOW = V + 32
 PIECE = U // 2
-SCALAR_COLUMNS = ((64, 48), (0, 64))
+SCALAR_COLUMNS = (56, 48)
 
 
 def tile_picked_ycnp_tanh_p_kernel(
@@ -130,20 +130,15 @@ def tile_picked_ycnp_tanh_p_kernel(
 
         h_ps = [ps.tile([P, 2, S // 2], F32, name="h_ps%d" % b) for b in range(4)]
         for g in range(PASSES):
-            src = w1_raw[g][:].rearrange("p j (c t) -> p c j t", t=PACK)
             last = g == PASSES - 1
-            pair = [
-                tile([P, 2, P, PACK], BF16, "w1_pair%d_0" % g, after="w1_pair0_1" if last else None),
-                tile([P, 2, P, PACK], BF16, "w1_pair%d_1" % g),
-            ]
-            dst = [pair[u][:].rearrange("p t c j -> p c j t") for u in range(2)]
+            src = w1_raw[g][:].rearrange("p j (c t) -> p c j t", t=PACK)
+            grouped = tile([P, PACK, P, PACK], BF16, "w1_grouped%d" % g, after="w1_grouped0")
+            dst = grouped[:].rearrange("p t c j -> p c j t")
+            share = SCALAR_COLUMNS[g]
+            cast("scalar", dst[:, :share], src[:, :share])
+            cast("vector", dst[:, share:], src[:, share:])
             for u in range(2):
-                share = SCALAR_COLUMNS[g][u]
-                if share:
-                    cast("scalar", dst[u][:, :share], src[:, :share, :, 2 * u : 2 * u + 2])
-                cast("vector", dst[u][:, share:], src[:, share:, :, 2 * u : 2 * u + 2])
-            for u in range(2):
-                w1_q = quantize(pair[u][:].rearrange("p t c j -> p (t c j)"), 2 * P, "w1_%d_%d" % (g, u))
+                w1_q = quantize(grouped[:, 2 * u : 2 * u + 2].rearrange("p t c j -> p (t c j)"), 2 * P, "w1_%d_%d" % (g, u))
                 for i in range(2):
                     entries = slice(i * S // 2, (i + 1) * S // 2)
                     for e in range(2):

@@ -53,7 +53,7 @@ def tile_picked_ycnp_tanh_p_kernel(
 
         def cast(engine, dst, src):
             if engine == "scalar":
-                nc.scalar.activation(dst, src, ACT.Copy)
+                nc.scalar.copy(dst, src)
             else:
                 nc.vector.tensor_copy(dst, src)
 
@@ -135,7 +135,10 @@ def tile_picked_ycnp_tanh_p_kernel(
             grouped = tile([P, PACK, P, PACK], BF16, "w1_grouped%d" % g, after="w1_grouped0")
             dst = grouped[:].rearrange("p t c j -> p c j t")
             share = SCALAR_COLUMNS[g]
-            cast("scalar", dst[:, :share], src[:, :share])
+            if last:
+                cast("scalar", dst[:, :share], src[:, :share])
+            else:
+                nc.scalar.activation(dst[:, :share], src[:, :share], ACT.Copy)
             cast("vector", dst[:, share:], src[:, share:])
             for u in range(2):
                 w1_q = quantize(grouped[:, 2 * u : 2 * u + 2].rearrange("p t c j -> p (t c j)"), 2 * P, "w1_%d_%d" % (g, u))
@@ -206,7 +209,7 @@ def tile_picked_ycnp_tanh_p_kernel(
         ]
         interleave("scalar", w2_half[0][:], w2_raw[:, :, halves[0]])
         y0_first = tile([P, PIECE], F32, "y0_first", after=1)
-        nc.scalar.activation(y0_first[:], y_ps[0][0][:, first], ACT.Copy)
+        nc.scalar.copy(y0_first[:], y_ps[0][0][:, first])
         interleave("scalar", w2_half[1][:], w2_raw[:, :, halves[1]])
 
         weave(0)
@@ -225,13 +228,13 @@ def tile_picked_ycnp_tanh_p_kernel(
             rr_product(bank[:], 0, i)
             nc.scalar.activation(rr[0][:, halves[i]], bank[:], ACT.Copy, scale=1.0 / D)
         y0_second = tile([P, PIECE], F32, "y0_second", after="w2_half0_codes")
-        nc.scalar.activation(y0_second[:], y_ps[0][0][:, second], ACT.Copy)
+        nc.scalar.copy(y0_second[:], y_ps[0][0][:, second])
         bank = ps.tile([P, V], F32, name="rr1_ps", tag="h_ps0")
         for i in range(2):
             rr_product(bank[:, halves[i]], 1, i)
         close_y(1)
         nc.scalar.activation(rr[1][:, :V], bank[:], ACT.Copy, scale=1.0 / D)
-        nc.scalar.activation(y1[:, first], y_ps[1][0][:], ACT.Copy)
+        nc.scalar.copy(y1[:, first], y_ps[1][0][:])
 
         def finish(m, cols, y_piece, after=None, after_tanh=None):
             width = cols.stop - cols.start
@@ -243,7 +246,7 @@ def tile_picked_ycnp_tanh_p_kernel(
             nc.sync.dma_start(out[halves[m], cols], result[:])
 
         finish(0, first, y0_first[:], after=2, after_tanh="w3_last1_codes")
-        nc.scalar.activation(y1[:, second], y_ps[1][1][:], ACT.Copy)
+        nc.scalar.copy(y1[:, second], y_ps[1][1][:])
         finish(0, second, y0_second[:])
         for cols in (first, slice(PIECE, U - P), slice(U - P, U)):
             finish(1, cols, y1[:, cols])

@@ -246,7 +246,14 @@ def tile_picked_ycnp_tanh_p_kernel(
             nc.sync.dma_start(out[halves[m], cols], result[:])
 
         finish(0, first, y0_first[:], after=2, after_tanh="w3_last1_codes")
-        nc.scalar.copy(y1[:, second], y_ps[1][1][:])
+        nc.scalar.copy(y1[:, PIECE : U - P], y_ps[1][1][:, :P])
+        fetched = tile([P, P], F32, "fetched")
+        nc.scalar.activation(fetched[:], rr[1][:].indirect(task_sb[:, (U - P) // LIST_ROWS :]), ACT.Copy)
         finish(0, second, y0_second[:])
-        for cols in (first, slice(PIECE, U - P), slice(U - P, U)):
+        for cols in (first, slice(PIECE, U - P)):
             finish(1, cols, y1[:, cols])
+        summed = tile([P, P], F32, "summed_last")
+        nc.vector.tensor_tensor(summed[:], y_ps[1][1][:, P:], fetched[:], ALU.add)
+        result = tile([P, P], F32, "result_last")
+        nc.scalar.activation(result[:], summed[:], ACT.Tanh)
+        nc.sync.dma_start(out[halves[1], U - P :], result[:])

@@ -20,6 +20,7 @@ PACK = 4
 K_PASS = P * PACK
 PASSES = K // K_PASS
 QUADRANTS = 4
+ALIGN = 256
 LIST_ROWS = 16
 M_TILES = N // P
 RR_WINDOW = V + 32
@@ -38,8 +39,8 @@ def tile_picked_ycnp_tanh_p_kernel(
 
         def tile(shape, dtype, name, after=None):
             if isinstance(after, int):
-                return shared.tile(shape, dtype, name=name, offset=after * 1024, align_bytes=64)
-            return sb.tile(shape, dtype, name=name, tag=after or name, align_bytes=64)
+                return shared.tile(shape, dtype, name=name, offset=after * 1024, align_bytes=ALIGN)
+            return sb.tile(shape, dtype, name=name, tag=after or name, align_bytes=ALIGN)
 
         def load_pass(w, g, name, after=None):
             raw = tile([P, PACK, w.shape[1]], F32, name, after)

@@ -25,7 +25,7 @@ LIST_ROWS = 16
 M_TILES = N // P
 RR_WINDOW = V + 32
 PIECE = U // 2
-SCALAR_COLUMNS = (56, 48)
+SCALAR_COLUMNS = (40, 48)
 
 
 def tile_picked_ycnp_tanh_p_kernel(

from contextlib import ExitStack

import concourse.mybir as mybir

K, T, S, H, N, D, V, U = 1024, 2048, 512, 512, 256, 2, 256, 512
FLOPS = 2 * (K * H * S + H * N * V + K * N * U)

F32 = mybir.dt.float32
BF16 = mybir.dt.bfloat16
I32 = mybir.dt.int32
U32 = mybir.dt.uint32
U16 = mybir.dt.uint16
U8 = mybir.dt.uint8
FP8X4 = mybir.dt.float8_e4m3fn_x4
ACT = mybir.ActivationFunctionType
ALU = mybir.AluOpType

P = 128
PACK = 4
K_PASS = P * PACK
PASSES = K // K_PASS
QUADRANTS = 4
ALIGN = 256
LIST_ROWS = 16
M_TILES = N // P
RR_WINDOW = V + 32
PIECE = U // 2
SCALAR_COLUMNS = (40, 48)


def tile_picked_ycnp_tanh_p_kernel(
    tc, x_words, x_scales, w1, w2, w3, offs, tgt, task, out
):
    nc = tc.nc
    with ExitStack() as ctx:
        sb = ctx.enter_context(tc.tile_pool(name="sb", bufs=1))
        shared = ctx.enter_context(tc.tile_pool(name="shared", bufs=1))
        ps = ctx.enter_context(tc.psum_pool(name="ps", bufs=1))

        def tile(shape, dtype, name, after=None):
            if isinstance(after, int):
                return shared.tile(shape, dtype, name=name, offset=after * 1024, align_bytes=ALIGN)
            return sb.tile(shape, dtype, name=name, tag=after or name, align_bytes=ALIGN)

        def load_pass(w, g, name, after=None):
            raw = tile([P, PACK, w.shape[1]], F32, name, after)
            nc.sync.dma_start(raw[:], w[g * K_PASS : (g + 1) * K_PASS, :].rearrange("(p j) c -> p j c", j=PACK))
            return raw

        def gather_words(window, offsets, name):
            picked = tile([P, S], U32, name)
            nc.vector.tensor_copy(picked[:], window[:].indirect(offsets[:]))
            return picked

        def cast(engine, dst, src):
            if engine == "scalar":
                nc.scalar.copy(dst, src)
            else:
                nc.vector.tensor_copy(dst, src)

        def interleave(engine, dst, src):
            cast(
                engine,
                dst.rearrange("p (c i) j -> p c j i", i=4),
                src.rearrange("p j (c i) -> p c j i", i=4),
            )

        def quantize(values, width, name, after=None):
            codes = tile([P, width], U32, name + "_codes", after)
            scales = tile([P, width], U8, name + "_scales")
            nc.vector.quantize_mx(out=codes[:].bitcast(FP8X4), scales=scales[:], in_=values)
            return codes, scales

        def quantize_tile(grouped, name, after=None):
            return quantize(grouped[:].rearrange("p c j -> p (c j)"), grouped.shape[1], name, after)

        def product(bank, weights, cols, words, word_scales, start=True, stop=True):
            codes, scales = weights
            nc.tensor.matmul_mx(
                out=bank,
                lhsT=codes[:, cols].bitcast(FP8X4),
                lhsT_scale=scales[:, cols],
                rhs=words.bitcast(FP8X4),
                rhs_scale=word_scales,
                start=start,
                stop=stop,
            )

        halves = [slice(0, P), slice(P, 2 * P)]

        offs_sb = tile([P, S // LIST_ROWS], U16, "offs_sb")
        tgt_sb = tile([P, U // LIST_ROWS], U16, "tgt_sb")
        task_sb = tile([P, U // LIST_ROWS], U16, "task_sb")
        table_scales = tile([P, T], U8, "table_scales")
        table_words = [tile([P, T], U32, "table_words0", after=0), tile([P, T], U32, "table_words1")]

        nc.sync.dma_start(table_scales[96:, :].bitcast(I32), x_scales.bitcast(I32).rearrange("g j c -> (g j) c"))
        nc.vector.memset(table_scales[:96, :].bitcast(I32), 0)
        nc.sync.dma_start(offs_sb[:], offs)
        nc.sync.dma_start(tgt_sb[:], tgt)
        for g in range(PASSES):
            words = x_words[g].rearrange("p c r -> p (c r)").bitcast(I32)
            nc.sync.dma_start(table_words[g][:].bitcast(I32), words)
        w1_raw = [load_pass(w1, 0, "w1_raw0")]

        picked_scales = tile([P, S + U], U8, "picked_scales")
        x_planes = [tile([P, S + U], U8, "x_planes%d" % g) for g in range(PASSES)]
        for g in range(PASSES):
            nc.vector.memset(x_planes[g][:].bitcast(I32), 0)
        rr = [tile([P, RR_WINDOW], F32, "rr%d" % m) for m in range(M_TILES)]
        for m in range(M_TILES):
            nc.vector.memset(rr[m][:, V:], 0.0)
        nc.vector.tensor_copy(picked_scales[:, :S], table_scales[:].indirect(offs_sb[:]))
        nc.vector.tensor_copy(picked_scales[:, S:], table_scales[:].indirect(tgt_sb[:]))

        def move_scales(g):
            for q in range(QUADRANTS):
                row = 96 + 16 * g + 4 * q
                rows = picked_scales[row : row + 4, :].bitcast(I32)
                nc.sync.dma_start(x_planes[g][32 * q + 4 * g : 32 * q + 4 * g + 4, :].bitcast(I32), rows)

        move_scales(0)
        w1_raw.append(load_pass(w1, 1, "w1_raw1", after="table_scales"))
        move_scales(1)

        ctx_words, tgt_words = [], []
        for g in range(PASSES):
            ctx_words.append(gather_words(table_words[g], offs_sb, "ctx_words%d" % g))
            tgt_words.append(gather_words(table_words[g], tgt_sb, "tgt_words%d" % g))
        w3_raw = [load_pass(w3, g, "w3_raw%d" % g, after=(0, "table_words1")[g]) for g in range(PASSES)]

        h_ps = [ps.tile([P, 2, S // 2], F32, name="h_ps%d" % b) for b in range(4)]
        for g in range(PASSES):
            last = g == PASSES - 1
            src = w1_raw[g][:].rearrange("p j (c t) -> p c j t", t=PACK)
            grouped = tile([P, PACK, P, PACK], BF16, "w1_grouped%d" % g, after="w1_grouped0")
            dst = grouped[:].rearrange("p t c j -> p c j t")
            share = SCALAR_COLUMNS[g]
            if last:
                cast("scalar", dst[:, :share], src[:, :share])
            else:
                nc.scalar.activation(dst[:, :share], src[:, :share], ACT.Copy)
            cast("vector", dst[:, share:], src[:, share:])
            for u in range(2):
                w1_q = quantize(grouped[:, 2 * u : 2 * u + 2].rearrange("p t c j -> p (t c j)"), 2 * P, "w1_%d_%d" % (g, u))
                for i in range(2):
                    entries = slice(i * S // 2, (i + 1) * S // 2)
                    for e in range(2):
                        product(
                            h_ps[2 * u + i][:, e],
                            w1_q,
                            halves[e],
                            ctx_words[g][:, entries],
                            x_planes[g][4 * g :, entries],
                            start=g == 0 and e == 0,
                            stop=last and e == 1,
                        )
        w2_raw = load_pass(w2, 0, "w2_raw", after="w1_raw0")
        nc.sync.dma_start(task_sb[:], task)

        first, second = slice(0, PIECE), slice(PIECE, U)
        y_pieces = [[slice(0, U)], [first, second]]
        y_ps = [
            [ps.tile([P, cols.stop - cols.start], F32, name="y_ps%d_%d" % (m, cols.start)) for cols in y_pieces[m]]
            for m in range(M_TILES)
        ]

        def y_pass(g, m, weights):
            for bank, cols in zip(y_ps[m], y_pieces[m]):
                planes = x_planes[g][4 * g :, S + cols.start : S + cols.stop]
                product(bank[:], weights, halves[0], tgt_words[g][:, cols], planes, start=g == 0, stop=g == 1)

        def close_y(m):
            y_pass(1, m, w3_last_q[m])

        def rr_product(bank, m, i):
            z_codes, z_scales = z_q[i]
            product(bank, w2_q[m], halves[0], z_codes[:], z_scales[:])

        w3_first = [tile([P, P, PACK], BF16, "w3_first%d" % m) for m in range(M_TILES)]
        for m in range(M_TILES):
            interleave("scalar", w3_first[m][:], w3_raw[0][:, :, halves[m]])
        for m in range(M_TILES):
            w3_first_q = quantize_tile(w3_first[m], "w3_first%d" % m)
            y_pass(0, m, w3_first_q)
        w3_last = [tile([P, P, PACK], BF16, "w3_last0", after="w3_first0")]
        interleave("vector", w3_last[0][:], w3_raw[1][:, :, halves[0]])

        z_pairs = [tile([P, 2, P, 2], BF16, "z_pairs%d" % i) for i in range(2)]
        z_half = [tile([P, P, PACK], BF16, "z_half%d" % i) for i in range(2)]

        def weave(i):
            dst = z_half[i][:].rearrange("p c j -> p (c j)").bitcast(I32).rearrange("p (c n u) -> p c u n", n=2, u=2)
            src = z_pairs[i][:].rearrange("p u c e -> p (u c e)").bitcast(I32)
            nc.vector.tensor_copy(dst, src.rearrange("p (u c n) -> p c u n", u=2, n=2))

        for b in range(4):
            u, i = divmod(b, 2)
            columns = h_ps[b][:].rearrange("p e (v d) -> p d v e", d=D)
            odd = tile([P, P, 2], F32, "odd%d" % b, after=b)
            nc.scalar.activation(odd[:], columns[:, 1], ACT.Relu)
            nc.vector.scalar_tensor_tensor(z_pairs[i][:, u], columns[:, 0], 0.0, odd[:], ALU.max, ALU.add)
            if b == 0:
                w3_last_q = [quantize_tile(w3_last[0], "w3_last0")]
                close_y(0)

        w2_half = [
            tile([P, P, PACK], BF16, "w2_half0", after=0),
            tile([P, P, PACK], BF16, "w2_half1", after=2),
        ]
        interleave("scalar", w2_half[0][:], w2_raw[:, :, halves[0]])
        y0_first = tile([P, PIECE], F32, "y0_first", after=1)
        nc.scalar.copy(y0_first[:], y_ps[0][0][:, first])
        interleave("scalar", w2_half[1][:], w2_raw[:, :, halves[1]])

        weave(0)
        weave(1)
        z_q = [quantize_tile(z_half[0], "z_half0")]
        w2_q = [quantize_tile(w2_half[0], "w2_half0")]
        z_q.append(quantize_tile(z_half[1], "z_half1"))
        w3_last.append(tile([P, P, PACK], BF16, "w3_last1", after=0))
        interleave("vector", w3_last[1][:], w3_raw[1][:, :, halves[1]])
        w2_q.append(quantize_tile(w2_half[1], "w2_half1"))
        w3_last_q.append(quantize_tile(w3_last[1], "w3_last1"))

        y1 = tile([P, U], F32, "y1")
        for i in range(2):
            bank = ps.tile([P, P], F32, name="rr0_ps%d" % i, tag="h_ps%d" % (i + 1))
            rr_product(bank[:], 0, i)
            nc.scalar.activation(rr[0][:, halves[i]], bank[:], ACT.Copy, scale=1.0 / D)
        y0_second = tile([P, PIECE], F32, "y0_second", after="w2_half0_codes")
        nc.scalar.copy(y0_second[:], y_ps[0][0][:, second])
        bank = ps.tile([P, V], F32, name="rr1_ps", tag="h_ps0")
        for i in range(2):
            rr_product(bank[:, halves[i]], 1, i)
        close_y(1)
        nc.scalar.activation(rr[1][:, :V], bank[:], ACT.Copy, scale=1.0 / D)
        nc.scalar.copy(y1[:, first], y_ps[1][0][:])

        def finish(m, cols, y_piece, after=None, after_tanh=None):
            width = cols.stop - cols.start
            offsets = task_sb[:, cols.start // LIST_ROWS : cols.stop // LIST_ROWS]
            summed = tile([P, width], F32, "summed%d_%d" % (m, cols.start), after)
            nc.vector.tensor_tensor(summed[:], rr[m][:].indirect(offsets), y_piece, ALU.add)
            result = tile([P, width], F32, "result%d_%d" % (m, cols.start), after_tanh)
            nc.scalar.activation(result[:], summed[:], ACT.Tanh)
            nc.sync.dma_start(out[halves[m], cols], result[:])

        finish(0, first, y0_first[:], after=2, after_tanh="w3_last1_codes")
        nc.scalar.copy(y1[:, PIECE : U - P], y_ps[1][1][:, :P])
        fetched = tile([P, P], F32, "fetched")
        nc.scalar.activation(fetched[:], rr[1][:].indirect(task_sb[:, (U - P) // LIST_ROWS :]), ACT.Copy)
        finish(0, second, y0_second[:])
        for cols in (first, slice(PIECE, U - P)):
            finish(1, cols, y1[:, cols])
        summed = tile([P, P], F32, "summed_last")
        nc.vector.tensor_tensor(summed[:], y_ps[1][1][:, P:], fetched[:], ALU.add)
        result = tile([P, P], F32, "result_last")
        nc.scalar.activation(result[:], summed[:], ACT.Tanh)
        nc.sync.dma_start(out[halves[1], U - P :], result[:])
